import numpy as np
import ml_dtypes


def mxq(x, axis, fmt="e4m3"):
    dtype, down = {"e4m3": (ml_dtypes.float8_e4m3fn, 7), "e5m2": (ml_dtypes.float8_e5m2, 14)}[fmt]
    v = np.moveaxis(np.asarray(x, np.float32).astype(ml_dtypes.bfloat16).astype(np.float64), axis, -1)
    blocks = v.reshape(v.shape[:-1] + (-1, 32))
    amax = np.abs(blocks).max(-1, keepdims=True)
    byte = np.maximum(np.where(amax > 0, np.frexp(amax)[1] - 1 + 127, 0) - down, 1)
    scale = np.exp2(byte - 127.0)
    codes = (blocks / scale).astype(np.float32).astype(dtype).astype(np.float64)
    return np.moveaxis((codes * scale).reshape(v.shape), -1, axis)


WIDE = False


def mx_kscale(k):
    if not WIDE:
        return np.ones(k)
    levels = np.array([10, -10, 5, -5, 0])
    if k % 512:
        return np.exp2(np.random.permutation(np.resize(levels, k // 32))).repeat(32)
    a = np.empty((k // 512, 16))
    for p in range(k // 512):
        a[p, :8] = np.random.permutation(np.resize(levels, 8))
        for g in range(8):
            far = levels[np.abs(levels - a[p, g]) >= 10]
            a[p, g + 8] = far[np.random.randint(len(far))]
    return np.exp2(a.ravel()).repeat(32)


def f64(x):
    return np.asarray(x).astype(np.float64)


def striped(idx):
    return np.tile(idx.reshape(-1, 16).T, (8, 1)).astype(np.uint16)


def unstriped(offs):
    return offs[:16].T.reshape(-1).astype(np.int64)


E2M1 = np.array([0.0, 0.5, 1.0, 1.5, 2.0, 3.0, 4.0, 6.0, -0.0, -0.5, -1.0, -1.5, -2.0, -3.0, -4.0, -6.0])


def pack_weight(w, fmt):
    k, n = w.shape
    w = f64(np.asarray(w, np.float32).astype(ml_dtypes.bfloat16)).reshape(k // 32, 32, n)
    amax = np.abs(w).max(1)
    if fmt == "e4m3":
        byte = np.frexp(amax)[1] - 1 + 127 - 7
    else:
        mant, ex = np.frexp(amax / 6.0)
        byte = np.where(mant > 0.5, ex, ex - 1) + 127
    byte = np.clip(np.where(amax > 0, byte, 1), 1, 254)
    scaled = (w * np.exp2(127.0 - byte)[:, None, :]).reshape(k, n).astype(np.float32)
    by_word = np.ascontiguousarray(scaled.reshape(k // 512, 128, 4, n).transpose(0, 1, 3, 2))
    if fmt == "e4m3":
        words = by_word.astype(ml_dtypes.float8_e4m3fn).view(np.uint8)
    else:
        c = by_word.astype(ml_dtypes.float4_e2m1fn).view(np.uint8) & 0xF
        words = (c[..., 0::2] | (c[..., 1::2] << 4)).reshape(k // 512, 128, 2 * n)
    return np.ascontiguousarray(words), np.ascontiguousarray(byte.astype(np.uint8).reshape(k // 512, 16, n))


def unpack_weight(words, scales, fmt):
    g, _, n = scales.shape
    words = np.ascontiguousarray(words).reshape(g, 128, n, -1)
    if fmt == "e4m3":
        vals = words.view(ml_dtypes.float8_e4m3fn).astype(np.float64)
    else:
        nib = np.empty((g, 128, n, 4), np.uint8)
        nib[..., 0::2] = words & 0xF
        nib[..., 1::2] = words >> 4
        vals = E2M1[nib]
    vals = vals * np.repeat(np.exp2(scales.astype(np.float64) - 127.0), 8, axis=1)[..., None]
    return vals.transpose(0, 1, 3, 2).reshape(g * 512, n)


def gelu(v):
    return 0.5 * v * (1.0 + np.tanh(np.sqrt(2.0 / np.pi) * (v + 0.044715 * v**3)))


def bf(x):
    return np.asarray(x, np.float32).astype(ml_dtypes.bfloat16)


def planes(Y):
    n, m = Y.shape
    b = f64(bf(Y)).reshape(n // 32, 32, m)
    amax = np.abs(b).max(1)
    byte = np.clip(np.where(amax > 0, np.frexp(amax)[1] - 1 + 127 - 7, 1), 1, 254)
    codes = (b * np.exp2(127.0 - byte)[:, None, :]).reshape(n, m).astype(np.float32).astype(ml_dtypes.float8_e4m3fn).view(np.uint8)
    words = codes.reshape(n // 512, 128, 4, m).transpose(0, 1, 3, 2)
    return np.ascontiguousarray(words), np.ascontiguousarray(byte.astype(np.uint8).reshape(n // 512, 16, m))


K, H, N, T, S, P = 512, 1024, 512, 4096, 1024, 512

def setup_inputs():
    n = np.random.standard_normal
    s = mx_kscale(K)[:, None]
    u = mx_kscale(H)[:, None]
    tab_words, tab_scales = pack_weight(n((K, T)) * s, "e4m3")
    w2_words, w2_scales = pack_weight(n((K, H)) / s / np.sqrt(K), "e2m1")
    wb_words, wb_scales = pack_weight(n((K, N)) / s / np.sqrt(K), "e4m3")
    return {
        "tab_words": tab_words, "tab_scales": tab_scales,
        "offs": striped(np.random.permutation(T)[:S]),
        "pos1": striped(np.random.permutation(S)[:P]),
        "pos2": striped(np.random.permutation(S)[:P]),
        "w1": (n((K, H)) / s * u.T / np.sqrt(K)).astype(np.float32),
        "w2_words": w2_words, "w2_scales": w2_scales,
        "base": (0.7 * n((H, S)) * u).astype(np.float32),
        "wa": (0.62 * n((H, N)) / u / np.sqrt(H)).astype(np.float32),
        "wb_words": wb_words, "wb_scales": wb_scales,
        "temp": np.random.uniform(0.4, 1.6, N).astype(np.float32),
        "dust": (0.7 * n(N)).astype(np.float32),
        "obs": (3.0 * np.exp(0.8 * n(N))[:, None] * n((N, P))).astype(np.float32),
    }

def reference(tab_words, tab_scales, offs, pos1, pos2, w1, w2_words, w2_scales, base, wa, wb_words, wb_scales, temp, dust, obs):
    v = unpack_weight(tab_words, tab_scales, "e4m3")[:, unstriped(offs)]
    w2 = unpack_weight(w2_words, w2_scales, "e2m1")
    wb = unpack_weight(wb_words, wb_scales, "e4m3")
    h = (mxq(f64(w1), 0, "e4m3").T @ v) * (w2.T @ v) + f64(base)
    e = mxq(f64(wa), 0, "e4m3").T @ mxq(h, 0, "e4m3")
    d = wb.T @ v
    top = e.max(axis=1)
    a = np.exp(f64(temp)[:, None] * (e[:, unstriped(pos1)] - top[:, None]))
    c = d[:, unstriped(pos2)] + f64(dust)[:, None]
    y = c * a * f64(obs)
    words, scales = planes(y)
    return y, words, scales

@@ -1,0 +1,253 @@
+from contextlib import ExitStack
+
+import concourse.mybir as mybir
+
+K, H, N, T, S, M = 512, 1024, 512, 4096, 1024, 512
+FLOPS = 2 * (2 * K * H * S + H * N * S + K * N * S)
+
+F32 = mybir.dt.float32
+BF16 = mybir.dt.bfloat16
+I32 = mybir.dt.int32
+U32 = mybir.dt.uint32
+U16 = mybir.dt.uint16
+U8 = mybir.dt.uint8
+FP8X4 = mybir.dt.float8_e4m3fn_x4
+FP4X4 = mybir.dt.float4_e2m1fn_x4
+ALU = mybir.AluOpType
+ACT = mybir.ActivationFunctionType
+
+P = 128
+W = 512
+G_ADD = [0,0,0,0]
+WA_ENG = "s"
+CO = "v"
+
+
+def tile_list_coma_outburst_scores_kernel(
+    tc, tab_words, tab_scales, offs, pos1, pos2, w1, w2_words, w2_scales, base, wa,
+    wb_words, wb_scales, temp, dust, obs, out_0, out_1, out_2,
+):
+    nc = tc.nc
+    with ExitStack() as ctx:
+        keep = ctx.enter_context(tc.tile_pool(name="keep", bufs=1))
+        stage = ctx.enter_context(tc.tile_pool(name="stage", bufs=1))
+        ring = ctx.enter_context(tc.tile_pool(name="ring", bufs=2))
+        psum = ctx.enter_context(tc.psum_pool(name="psum", bufs=2))
+
+        def scale_rows(engine, plane, rows):
+            for q in range(4):
+                engine.dma_start(out=plane[32 * q : 32 * q + 4, :].bitcast(I32), in_=rows[0, 4 * q : 4 * q + 4, :].bitcast(I32))
+
+        idx = keep.tile([P, S // 16], U16, name="idx")
+        p1 = keep.tile([P, M // 16], U16, name="p1")
+        p2 = keep.tile([P, M // 16], U16, name="p2")
+        R = 8192 + 512
+        tw = keep.tile([P, T], U32, name="tw", align_bytes=64)
+        ts = stage.tile([P, T], U8, name="ts", align_bytes=64, offset=5 * R - 2048)
+        w2w = stage.tile([P, 2 * H], U8, name="w2w", align_bytes=64, offset=3 * R - 1024)
+        wbw = stage.tile([P, N], U32, name="wbw", align_bytes=64, offset=R - 1024)
+        wbs = keep.tile([P, N], U8, name="wbs", align_bytes=64)
+
+        nc.vector.memset(ts[:].bitcast(I32), 0)
+        nc.gpsimd.memset(wbs[:].bitcast(I32), 0)
+
+        nc.sync.dma_start(idx[:], offs)
+        nc.sync.dma_start(p2[:], pos2)
+        nc.sync.dma_start(p1[:], pos1)
+        nc.sync.dma_start(out=wbw[:].bitcast(I32), in_=wb_words[0].rearrange("p n t -> p (n t)").bitcast(I32))
+        nc.sync.dma_start(out=tw[:].bitcast(I32), in_=tab_words[0].rearrange("p n t -> p (n t)").bitcast(I32))
+        nc.sync.dma_start(out=w2w[:].bitcast(I32), in_=w2_words[0].bitcast(I32))
+        scale_rows(nc.sync, ts, tab_scales)
+        scale_rows(nc.gpsimd, wbs, wb_scales)
+
+        def load_rows(rows, name, region, shift=0):
+            raw = stage.tile([P, 4, W], F32, name=name, align_bytes=64, offset=region * R + shift)
+            nc.sync.dma_start(out=raw[:], in_=rows.rearrange("(p j) c -> p j c", j=4))
+            return raw
+
+        def load_base(b, h, region, shift=0):
+            return load_rows(base[W * b : W * (b + 1), W * h : W * (h + 1)], "base%d%d" % (b, h), region, shift)
+
+        w1_raw = {}
+        wa_raw = {}
+        base_sb = {}
+
+        gw = [keep.tile([P, W], U32, name="gw%d" % h, align_bytes=64) for h in range(2)]
+        gs = {0: keep.tile([P, W], U8, name="gs0", align_bytes=64)}
+
+        def gather_table(h):
+            cols = idx[:, 32 * h : 32 * (h + 1)]
+            nc.vector.tensor_copy(out=gw[h][:], in_=tw[:].indirect(cols))
+            nc.vector.tensor_copy(out=gs[h][:], in_=ts[:].indirect(cols))
+
+        wbw_d = keep.tile([P, N], U32, name="wbw_d", align_bytes=64)
+        wbs_d = keep.tile([P, N], U8, name="wbs_d", align_bytes=64)
+        w2w_d = keep.tile([P, 2 * H], U8, name="w2w_d", align_bytes=64)
+        w2s_d = keep.tile([P, H], U8, name="w2s_d", align_bytes=64)
+
+        nc.scalar.copy(out=wbw_d[:].rearrange("p (t m) -> p t m", t=4), in_=wbw[:].rearrange("p (m t) -> p t m", t=4))
+        w1_raw[0] = load_rows(w1[:, 0:W], "w1r0", 0)
+        w2s = stage.tile([P, H], U8, name="w2s", align_bytes=64, offset=R)
+        nc.vector.memset(w2s[:].bitcast(I32), 0)
+        scale_rows(nc.sync, w2s, w2_scales)
+        nc.scalar.copy(out=w2w_d[:].bitcast(U16).rearrange("p (b t m) -> p b t m", b=2, t=4), in_=w2w[:].bitcast(U16).rearrange("p (b m t) -> p b t m", b=2, t=4))
+        base_sb[0, 0] = load_base(0, 0, 2, 512)
+        base_sb[0, 1] = load_base(0, 1, 3)
+        nc.gpsimd.tensor_copy(out=wbs_d[:].rearrange("p (t m) -> p t m", t=4), in_=wbs[:].rearrange("p (m t) -> p t m", t=4))
+        temp_sb = keep.tile([P, 4], F32, name="temp_sb")
+        dust_sb = keep.tile([P, 4], F32, name="dust_sb")
+        nc.gpsimd.dma_start(out=dust_sb[:], in_=dust.rearrange("(p t) -> p t", t=4))
+        nc.gpsimd.dma_start(out=temp_sb[:], in_=temp.rearrange("(p t) -> p t", t=4))
+        gather_table(0)
+        for b in range(2):
+            nc.gpsimd.tensor_copy(out=w2s_d[:, W * b : W * (b + 1)].rearrange("p (t m) -> p t m", t=4), in_=w2s[:, W * b : W * (b + 1)].rearrange("p (m t) -> p t m", t=4))
+
+        def round_weight(raw, eng):
+            wbf = ring.tile([P, 4 * W], BF16, name="wbf", align_bytes=64)
+            o = wbf[:].rearrange("p (t m j) -> p m j t", t=4, j=4)
+            i = raw[:].rearrange("p j (m t) -> p m j t", t=4)
+            if eng == "s":
+                nc.scalar.copy(out=o, in_=i)
+            elif eng == "v":
+                nc.vector.tensor_copy(out=o, in_=i)
+            else:
+                nc.gpsimd.tensor_scalar(out=o, in0=i, scalar1=1.0, scalar2=0.0, op0=ALU.mult, op1=ALU.add)
+            return wbf
+
+        def quantise(src, name):
+            codes = keep.tile([P, W], U32, name=name + "_w", align_bytes=64)
+            scales = keep.tile([P, W], U8, name=name + "_s", align_bytes=64)
+            nc.vector.quantize_mx(out=codes[:].bitcast(FP8X4), scales=scales[:], in_=src[:])
+            return codes, scales
+
+        d = [keep.tile([P, S], F32, name="d%d" % t) for t in range(4)]
+        e = [keep.tile([P, S], F32, name="e%d" % t) for t in range(4)]
+        top = keep.tile([P, 8], F32, name="top")
+        bias = keep.tile([P, 4], F32, name="bias")
+
+        def d_half(h):
+            for t in range(4):
+                acc = psum.tile([P, W], F32, name="acc", bufs=4)
+                c = slice(P * t, P * (t + 1))
+                nc.tensor.matmul_mx(out=acc[:], lhsT=wbw_d[:, c].bitcast(FP8X4), lhsT_scale=wbs_d[:, c],
+                                    rhs=gw[h][:].bitcast(FP8X4), rhs_scale=gs[h][:], start=True, stop=True)
+                nc.scalar.copy(out=d[t][:, W * h : W * (h + 1)], in_=acc[:])
+
+        w1q = {}
+        waq = {}
+        hq = {}
+
+        def products(b, h):
+            prod = ring.tile([P, 4, W], F32, name="prod")
+            for t in range(4):
+                c = slice(P * t, P * (t + 1))
+                g0 = W * b + P * t
+                pb = psum.tile([P, W], F32, name="pb")
+                nc.tensor.matmul_mx(out=pb[:], lhsT=w2w_d[:, 2 * g0 : 2 * (g0 + P)].bitcast(FP4X4), lhsT_scale=w2s_d[:, g0 : g0 + P],
+                                    rhs=gw[h][:].bitcast(FP8X4), rhs_scale=gs[h][:], start=True, stop=True)
+                pa = psum.tile([P, W], F32, name="pa")
+                nc.tensor.matmul_mx(out=pa[:], lhsT=w1q[b][0][:, c].bitcast(FP8X4), lhsT_scale=w1q[b][1][:, c],
+                                    rhs=gw[h][:].bitcast(FP8X4), rhs_scale=gs[h][:], start=True, stop=True)
+                pb_sb = ring.tile([P, W], F32, name="pb_sb", bufs=3)
+                nc.scalar.copy(out=pb_sb[:], in_=pb[:])
+                nc.vector.tensor_tensor(out=prod[:, t, :], in0=pa[:], in1=pb_sb[:], op=ALU.mult)
+            return prod
+
+        def finish(b, h, prod):
+            hb = ring.tile([P, 4 * W], BF16, name="hb", align_bytes=64)
+            cut = G_ADD[2 * h + b]
+            for eng, j0, j1 in [(nc.gpsimd, j, j + 128) for j in range(0, cut, 128)] + [(nc.vector, cut, W)]:
+                if j1 > j0:
+                    eng.tensor_tensor(
+                        out=hb[:, 4 * j0 : 4 * j1].rearrange("p (c i t) -> p c t i", i=4, t=4),
+                        in0=prod[:, :, j0:j1].rearrange("p t (c i) -> p c t i", i=4),
+                        in1=base_sb[b, h][:, :, j0:j1].rearrange("p t (c i) -> p c t i", i=4),
+                        op=ALU.add,
+                    )
+            hq[b, h] = quantise(hb, "h%d%d" % (b, h))
+
+        def e_tile(h, t):
+            acc = psum.tile([P, W], F32, name="acc", bufs=4)
+            c = slice(P * t, P * (t + 1))
+            for b in range(2):
+                nc.tensor.matmul_mx(out=acc[:], lhsT=waq[b][0][:, c].bitcast(FP8X4), lhsT_scale=waq[b][1][:, c],
+                                    rhs=hq[b, h][0][:].bitcast(FP8X4), rhs_scale=hq[b, h][1][:], start=(b == 0), stop=(b == 1))
+            nc.vector.tensor_scalar(out=e[t][:, W * h : W * (h + 1)], in0=acc[:], scalar1=1.0,
+                                    scalar2=(top[:, t : t + 1] if h else None), op0=ALU.mult, op1=ALU.max,
+                                    accum_out=top[:, 4 * h + t : 4 * h + t + 1])
+
+        def dust_tile(t):
+            dg = ring.tile([P, M], F32, name="dg")
+            nc.vector.tensor_copy(out=dg[:], in_=d[t][:].indirect(p2[:]))
+            if CO == "v":
+                nc.vector.scalar_tensor_tensor(out=yt[:, t, :], in0=dg[:], scalar=dust_sb[:, t : t + 1], in1=yt[:, t, :],
+                                               op0=ALU.add, op1=ALU.mult)
+            else:
+                cg = ring.tile([P, M], F32, name="cg")
+                nc.scalar.activation(out=cg[:], in_=dg[:], func=ACT.Identity, bias=dust_sb[:, t : t + 1])
+                nc.gpsimd.tensor_tensor(out=yt[:, t, :], in0=cg[:], in1=yt[:, t, :], op=ALU.mult)
+
+        wbf0 = ring.tile([P, 4 * W], BF16, name="wbf", align_bytes=64)
+        c0 = keep.tile([P, W], U32, name="w10_w", align_bytes=64)
+        s0 = keep.tile([P, W], U8, name="w10_s", align_bytes=64)
+        for u in range(2):
+            nc.scalar.copy(out=wbf0[:, 2 * W * u : 2 * W * (u + 1)].rearrange("p (t m j) -> p m j t", t=2, j=4),
+                           in_=w1_raw[0][:].rearrange("p j (m t) -> p m j t", t=4)[:, :, :, 2 * u : 2 * u + 2])
+            nc.vector.quantize_mx(out=c0[:, 256 * u : 256 * (u + 1)].bitcast(FP8X4), scales=s0[:, 256 * u : 256 * (u + 1)], in_=wbf0[:, 2 * W * u : 2 * W * (u + 1)])
+        w1q[0] = (c0, s0)
+        gs[1] = stage.tile([P, W], U8, name="gs1", align_bytes=64, offset=0)
+        gather_table(1)
+        w1_raw[1] = load_rows(w1[:, W : 2 * W], "w1r1", 0, 512)
+        base_sb[1, 0] = load_base(1, 0, 1)
+        wa_raw[0] = load_rows(wa[0:W, :], "war0", 4)
+        wa_raw[1] = load_rows(wa[W : 2 * W, :], "war1", 5)
+        prod00 = products(0, 0)
+        prod01 = products(0, 1)
+        finish(0, 0, prod00)
+        base_sb[1, 1] = load_base(1, 1, 2, 512)
+        d_half(0)
+        w1q[1] = quantise(round_weight(w1_raw[1], "s"), "w11")
+        yt = load_rows(obs, "yt", 0, 512)
+        finish(0, 1, prod01)
+        prod10 = products(1, 0)
+        d_half(1)
+        waq[0] = quantise(round_weight(wa_raw[0], WA_ENG), "wa0")
+        waq[1] = quantise(round_weight(wa_raw[1], WA_ENG), "wa1")
+        finish(1, 0, prod10)
+        prod11 = products(1, 1)
+        for t in range(4):
+            dust_tile(t)
+        for t in range(4):
+            e_tile(0, t)
+        finish(1, 1, prod11)
+
+        yb = keep.tile([P, 4 * M], BF16, name="yb", align_bytes=64)
+        yw = keep.tile([P, M], U32, name="yw", align_bytes=64)
+        ys = keep.tile([P, M], U8, name="ys", align_bytes=64)
+        y_rows = out_0.rearrange("(p t) m -> p t m", t=4)
+        words_out = out_1[0].rearrange("p m t -> p (m t)").bitcast(I32)
+
+        def look(t, m0, m1):
+            a = ring.tile([P, m1 - m0], F32, name="a", bufs=8)
+            nc.scalar.activation(out=a[:], in_=e[t][:].indirect(p1[:, m0 // 16 : m1 // 16]), func=ACT.Exp,
+                                 bias=bias[:, t : t + 1], scale=temp_sb[:, t : t + 1])
+            nc.vector.tensor_tensor(out=yt[:, t, m0:m1], in0=yt[:, t, m0:m1], in1=a[:], op=ALU.mult)
+
+        def planes(m0, m1):
+            nc.sync.dma_start(out=y_rows[:, :, m0:m1], in_=yt[:, :, m0:m1])
+            nc.vector.tensor_copy(out=yb[:, 4 * m0 : 4 * m1].rearrange("p (c i t) -> p c t i", i=4, t=4),
+                                  in_=yt[:, :, m0:m1].rearrange("p t (c i) -> p c t i", i=4))
+            nc.vector.quantize_mx(out=yw[:, m0:m1].bitcast(FP8X4), scales=ys[:, m0:m1], in_=yb[:, 4 * m0 : 4 * m1])
+            nc.sync.dma_start(out=words_out[:, m0:m1], in_=yw[:, m0:m1].bitcast(I32))
+
+        for t in range(4):
+            e_tile(1, t)
+            nc.gpsimd.tensor_scalar(out=bias[:, t : t + 1], in0=top[:, 4 + t : 5 + t], scalar1=temp_sb[:, t : t + 1],
+                                    scalar2=-1.0, op0=ALU.mult, op1=ALU.mult)
+        for m0 in (0, M // 2):
+            for t in range(4):
+                look(t, m0, m0 + M // 2)
+            planes(m0, m0 + M // 2)
+        for q in range(4):
+            eng = nc.scalar if q % 2 else nc.sync
+            eng.dma_start(out=out_2[0, 4 * q : 4 * q + 4, :].bitcast(I32), in_=ys[32 * q : 32 * q + 4, :].bitcast(I32))

@@ -85,7 +85,7 @@ def tile_list_coma_outburst_scores_kernel(
         w2w_d = keep.tile([P, 2 * H], U8, name="w2w_d", align_bytes=64)
         w2s_d = keep.tile([P, H], U8, name="w2s_d", align_bytes=64)
 
-        nc.scalar.copy(out=wbw_d[:].rearrange("p (t m) -> p t m", t=4), in_=wbw[:].rearrange("p (m t) -> p t m", t=4))
+        nc.scalar.copy(out=wbw_d[:].rearrange("p (u e m) -> p u m e", u=2, e=2), in_=wbw[:].rearrange("p (m u e) -> p u m e", u=2, e=2))
         w1_raw[0] = load_rows(w1[:, 0:W], "w1r0", 0)
         w2s = stage.tile([P, H], U8, name="w2s", align_bytes=64, offset=R)
         nc.vector.memset(w2s[:].bitcast(I32), 0)
@@ -104,8 +104,8 @@ def tile_list_coma_outburst_scores_kernel(
 
         def round_weight(raw, eng):
             wbf = ring.tile([P, 4 * W], BF16, name="wbf", align_bytes=64)
-            o = wbf[:].rearrange("p (t m j) -> p m j t", t=4, j=4)
-            i = raw[:].rearrange("p j (m t) -> p m j t", t=4)
+            o = wbf[:].rearrange("p (u e m j) -> p u m j e", u=2, e=2, j=4)
+            i = raw[:].rearrange("p j (m u e) -> p u m j e", u=2, e=2)
             if eng == "s":
                 nc.scalar.copy(out=o, in_=i)
             elif eng == "v":
@@ -127,7 +127,7 @@ def tile_list_coma_outburst_scores_kernel(
 
         def d_half(h):
             for t in range(4):
-                acc = psum.tile([P, W], F32, name="acc", bufs=4)
+                acc = psum.tile([P, W], F32, name="acc", bufs=2)
                 c = slice(P * t, P * (t + 1))
                 nc.tensor.matmul_mx(out=acc[:], lhsT=wbw_d[:, c].bitcast(FP8X4), lhsT_scale=wbs_d[:, c],
                                     rhs=gw[h][:].bitcast(FP8X4), rhs_scale=gs[h][:], start=True, stop=True)
@@ -145,7 +145,7 @@ def tile_list_coma_outburst_scores_kernel(
                 pb = psum.tile([P, W], F32, name="pb")
                 nc.tensor.matmul_mx(out=pb[:], lhsT=w2w_d[:, 2 * g0 : 2 * (g0 + P)].bitcast(FP4X4), lhsT_scale=w2s_d[:, g0 : g0 + P],
                                     rhs=gw[h][:].bitcast(FP8X4), rhs_scale=gs[h][:], start=True, stop=True)
-                pa = psum.tile([P, W], F32, name="pa")
+                pa = psum.tile([P, W], F32, name="pa", bufs=4)
                 nc.tensor.matmul_mx(out=pa[:], lhsT=w1q[b][0][:, c].bitcast(FP8X4), lhsT_scale=w1q[b][1][:, c],
                                     rhs=gw[h][:].bitcast(FP8X4), rhs_scale=gs[h][:], start=True, stop=True)
                 pb_sb = ring.tile([P, W], F32, name="pb_sb", bufs=3)
@@ -159,15 +159,15 @@ def tile_list_coma_outburst_scores_kernel(
             for eng, j0, j1 in [(nc.gpsimd, j, j + 128) for j in range(0, cut, 128)] + [(nc.vector, cut, W)]:
                 if j1 > j0:
                     eng.tensor_tensor(
-                        out=hb[:, 4 * j0 : 4 * j1].rearrange("p (c i t) -> p c t i", i=4, t=4),
-                        in0=prod[:, :, j0:j1].rearrange("p t (c i) -> p c t i", i=4),
-                        in1=base_sb[b, h][:, :, j0:j1].rearrange("p t (c i) -> p c t i", i=4),
+                        out=hb[:, 4 * j0 : 4 * j1].rearrange("p (c i t) -> p c t i", i=2, t=4),
+                        in0=prod[:, :, j0:j1].rearrange("p t (c i) -> p c t i", i=2),
+                        in1=base_sb[b, h][:, :, j0:j1].rearrange("p t (c i) -> p c t i", i=2),
                         op=ALU.add,
                     )
             hq[b, h] = quantise(hb, "h%d%d" % (b, h))
 
         def e_tile(h, t):
-            acc = psum.tile([P, W], F32, name="acc", bufs=4)
+            acc = psum.tile([P, W], F32, name="pa", bufs=4) if h else psum.tile([P, W], F32, name="acc", bufs=2)
             c = slice(P * t, P * (t + 1))
             for b in range(2):
                 nc.tensor.matmul_mx(out=acc[:], lhsT=waq[b][0][:, c].bitcast(FP8X4), lhsT_scale=waq[b][1][:, c],
@@ -176,22 +176,21 @@ def tile_list_coma_outburst_scores_kernel(
                                     scalar2=(top[:, t : t + 1] if h else None), op0=ALU.mult, op1=ALU.max,
                                     accum_out=top[:, 4 * h + t : 4 * h + t + 1])
 
-        def dust_tile(t):
-            dg = ring.tile([P, M], F32, name="dg")
-            nc.vector.tensor_copy(out=dg[:], in_=d[t][:].indirect(p2[:]))
-            if CO == "v":
-                nc.vector.scalar_tensor_tensor(out=yt[:, t, :], in0=dg[:], scalar=dust_sb[:, t : t + 1], in1=yt[:, t, :],
-                                               op0=ALU.add, op1=ALU.mult)
-            else:
-                cg = ring.tile([P, M], F32, name="cg")
-                nc.scalar.activation(out=cg[:], in_=dg[:], func=ACT.Identity, bias=dust_sb[:, t : t + 1])
-                nc.gpsimd.tensor_tensor(out=yt[:, t, :], in0=cg[:], in1=yt[:, t, :], op=ALU.mult)
+        dg = {}
+
+        def pick(t, m0, m1):
+            dg[t, m0] = keep.tile([P, m1 - m0], F32, name="dg%d_%d" % (t, m0))
+            nc.vector.tensor_copy(out=dg[t, m0][:], in_=d[t][:].indirect(p2[:, m0 // 16 : m1 // 16]))
+
+        def weigh(t, m0, m1, g0):
+            nc.vector.scalar_tensor_tensor(out=yt[:, t, m0:m1], in0=dg[t, g0][:, m0 - g0 : m1 - g0], scalar=dust_sb[:, t : t + 1], in1=yt[:, t, m0:m1],
+                                           op0=ALU.add, op1=ALU.mult)
 
         wbf0 = ring.tile([P, 4 * W], BF16, name="wbf", align_bytes=64)
         c0 = keep.tile([P, W], U32, name="w10_w", align_bytes=64)
         s0 = keep.tile([P, W], U8, name="w10_s", align_bytes=64)
         for u in range(2):
-            nc.scalar.copy(out=wbf0[:, 2 * W * u : 2 * W * (u + 1)].rearrange("p (t m j) -> p m j t", t=2, j=4),
+            (nc.vector.tensor_copy if u else nc.scalar.copy)(out=wbf0[:, 2 * W * u : 2 * W * (u + 1)].rearrange("p (t m j) -> p m j t", t=2, j=4),
                            in_=w1_raw[0][:].rearrange("p j (m t) -> p m j t", t=4)[:, :, :, 2 * u : 2 * u + 2])
             nc.vector.quantize_mx(out=c0[:, 256 * u : 256 * (u + 1)].bitcast(FP8X4), scales=s0[:, 256 * u : 256 * (u + 1)], in_=wbf0[:, 2 * W * u : 2 * W * (u + 1)])
         w1q[0] = (c0, s0)
@@ -216,7 +215,8 @@ def tile_list_coma_outburst_scores_kernel(
         finish(1, 0, prod10)
         prod11 = products(1, 1)
         for t in range(4):
-            dust_tile(t)
+            pick(t, 0, M)
+            weigh(t, 0, M, 0)
         for t in range(4):
             e_tile(0, t)
         finish(1, 1, prod11)
@@ -235,8 +235,8 @@ def tile_list_coma_outburst_scores_kernel(
 
         def planes(m0, m1):
             nc.sync.dma_start(out=y_rows[:, :, m0:m1], in_=yt[:, :, m0:m1])
-            nc.vector.tensor_copy(out=yb[:, 4 * m0 : 4 * m1].rearrange("p (c i t) -> p c t i", i=4, t=4),
-                                  in_=yt[:, :, m0:m1].rearrange("p t (c i) -> p c t i", i=4))
+            nc.vector.tensor_copy(out=yb[:, 4 * m0 : 4 * m1].rearrange("p (c i t) -> p c t i", i=2, t=4),
+                                  in_=yt[:, :, m0:m1].rearrange("p t (c i) -> p c t i", i=2))
             nc.vector.quantize_mx(out=yw[:, m0:m1].bitcast(FP8X4), scales=ys[:, m0:m1], in_=yb[:, 4 * m0 : 4 * m1])
             nc.sync.dma_start(out=words_out[:, m0:m1], in_=yw[:, m0:m1].bitcast(I32))
 

@@ -46,10 +46,10 @@ def tile_list_coma_outburst_scores_kernel(
         ts = stage.tile([P, T], U8, name="ts", align_bytes=64, offset=5 * R - 2048)
         w2w = stage.tile([P, 2 * H], U8, name="w2w", align_bytes=64, offset=3 * R - 1024)
         wbw = stage.tile([P, N], U32, name="wbw", align_bytes=64, offset=R - 1024)
-        wbs = keep.tile([P, N], U8, name="wbs", align_bytes=64)
+        w2s = stage.tile([P, H], U8, name="w2s", align_bytes=64, offset=6 * R)
 
         nc.vector.memset(ts[:].bitcast(I32), 0)
-        nc.gpsimd.memset(wbs[:].bitcast(I32), 0)
+        nc.gpsimd.memset(w2s[:].bitcast(I32), 0)
 
         nc.sync.dma_start(idx[:], offs)
         nc.sync.dma_start(p2[:], pos2)
@@ -58,7 +58,7 @@ def tile_list_coma_outburst_scores_kernel(
         nc.sync.dma_start(out=tw[:].bitcast(I32), in_=tab_words[0].rearrange("p n t -> p (n t)").bitcast(I32))
         nc.sync.dma_start(out=w2w[:].bitcast(I32), in_=w2_words[0].bitcast(I32))
         scale_rows(nc.sync, ts, tab_scales)
-        scale_rows(nc.gpsimd, wbs, wb_scales)
+        scale_rows(nc.gpsimd, w2s, w2_scales)
 
         def load_rows(rows, name, region, shift=0):
             raw = stage.tile([P, 4, W], F32, name=name, align_bytes=64, offset=region * R + shift)
@@ -87,20 +87,20 @@ def tile_list_coma_outburst_scores_kernel(
 
         nc.scalar.copy(out=wbw_d[:].rearrange("p (u e m) -> p u m e", u=2, e=2), in_=wbw[:].rearrange("p (m u e) -> p u m e", u=2, e=2))
         w1_raw[0] = load_rows(w1[:, 0:W], "w1r0", 0)
-        w2s = stage.tile([P, H], U8, name="w2s", align_bytes=64, offset=R)
-        nc.vector.memset(w2s[:].bitcast(I32), 0)
-        scale_rows(nc.sync, w2s, w2_scales)
+        wbs = stage.tile([P, N], U8, name="wbs", align_bytes=64, offset=R)
+        nc.vector.memset(wbs[:].bitcast(I32), 0)
+        scale_rows(nc.sync, wbs, wb_scales)
         nc.scalar.copy(out=w2w_d[:].bitcast(U16).rearrange("p (b t m) -> p b t m", b=2, t=4), in_=w2w[:].bitcast(U16).rearrange("p (b m t) -> p b t m", b=2, t=4))
         base_sb[0, 0] = load_base(0, 0, 2, 512)
-        base_sb[0, 1] = load_base(0, 1, 3)
+        w1_raw[1] = load_rows(w1[:, W : 2 * W], "w1r1", 3)
+        for b in range(2):
+            nc.gpsimd.tensor_copy(out=w2s_d[:, W * b : W * (b + 1)].rearrange("p (t m) -> p t m", t=4), in_=w2s[:, W * b : W * (b + 1)].rearrange("p (m t) -> p t m", t=4))
         nc.gpsimd.tensor_copy(out=wbs_d[:].rearrange("p (t m) -> p t m", t=4), in_=wbs[:].rearrange("p (m t) -> p t m", t=4))
-        temp_sb = keep.tile([P, 4], F32, name="temp_sb")
-        dust_sb = keep.tile([P, 4], F32, name="dust_sb")
+        temp_sb = stage.tile([P, 4], F32, name="temp_sb", align_bytes=64, offset=6 * R)
+        dust_sb = stage.tile([P, 4], F32, name="dust_sb", align_bytes=64, offset=6 * R + 64)
         nc.gpsimd.dma_start(out=dust_sb[:], in_=dust.rearrange("(p t) -> p t", t=4))
         nc.gpsimd.dma_start(out=temp_sb[:], in_=temp.rearrange("(p t) -> p t", t=4))
         gather_table(0)
-        for b in range(2):
-            nc.gpsimd.tensor_copy(out=w2s_d[:, W * b : W * (b + 1)].rearrange("p (t m) -> p t m", t=4), in_=w2s[:, W * b : W * (b + 1)].rearrange("p (m t) -> p t m", t=4))
 
         def round_weight(raw, eng):
             wbf = ring.tile([P, 4 * W], BF16, name="wbf", align_bytes=64)
@@ -117,18 +117,19 @@ def tile_list_coma_outburst_scores_kernel(
         def quantise(src, name):
             codes = keep.tile([P, W], U32, name=name + "_w", align_bytes=64)
             scales = keep.tile([P, W], U8, name=name + "_s", align_bytes=64)
-            nc.vector.quantize_mx(out=codes[:].bitcast(FP8X4), scales=scales[:], in_=src[:])
+            nc.vector.quantize_mx(out=codes[:].bitcast(FP8X4), scales=scales[:], in_=src[:, :])
             return codes, scales
 
-        d = [keep.tile([P, S], F32, name="d%d" % t) for t in range(4)]
+        d = {}
         e = [keep.tile([P, S], F32, name="e%d" % t) for t in range(4)]
         top = keep.tile([P, 8], F32, name="top")
         bias = keep.tile([P, 4], F32, name="bias")
 
-        def d_half(h):
-            for t in range(4):
-                acc = psum.tile([P, W], F32, name="acc", bufs=2)
-                c = slice(P * t, P * (t + 1))
+        def d_tile(t):
+            d[t] = stage.tile([P, S], F32, name="d%d" % t, align_bytes=64, offset=[512, 4608, 8 * R, 8 * R + 4096][t])
+            c = slice(P * t, P * (t + 1))
+            for h in range(2):
+                acc = psum.tile([P, W], F32, name="acc", bufs=3)
                 nc.tensor.matmul_mx(out=acc[:], lhsT=wbw_d[:, c].bitcast(FP8X4), lhsT_scale=wbs_d[:, c],
                                     rhs=gw[h][:].bitcast(FP8X4), rhs_scale=gs[h][:], start=True, stop=True)
                 nc.scalar.copy(out=d[t][:, W * h : W * (h + 1)], in_=acc[:])
@@ -138,17 +139,17 @@ def tile_list_coma_outburst_scores_kernel(
         hq = {}
 
         def products(b, h):
-            prod = ring.tile([P, 4, W], F32, name="prod")
+            prod = stage.tile([P, 4, W], F32, name="prod%d%d" % (b, h), align_bytes=64, offset=[7, 8, 7, 9][2 * b + h] * R)
             for t in range(4):
                 c = slice(P * t, P * (t + 1))
                 g0 = W * b + P * t
                 pb = psum.tile([P, W], F32, name="pb")
                 nc.tensor.matmul_mx(out=pb[:], lhsT=w2w_d[:, 2 * g0 : 2 * (g0 + P)].bitcast(FP4X4), lhsT_scale=w2s_d[:, g0 : g0 + P],
                                     rhs=gw[h][:].bitcast(FP8X4), rhs_scale=gs[h][:], start=True, stop=True)
-                pa = psum.tile([P, W], F32, name="pa", bufs=4)
+                pa = psum.tile([P, W], F32, name="pa", bufs=3)
                 nc.tensor.matmul_mx(out=pa[:], lhsT=w1q[b][0][:, c].bitcast(FP8X4), lhsT_scale=w1q[b][1][:, c],
                                     rhs=gw[h][:].bitcast(FP8X4), rhs_scale=gs[h][:], start=True, stop=True)
-                pb_sb = ring.tile([P, W], F32, name="pb_sb", bufs=3)
+                pb_sb = ring.tile([P, W], F32, name="pb_sb", bufs=4)
                 nc.scalar.copy(out=pb_sb[:], in_=pb[:])
                 nc.vector.tensor_tensor(out=prod[:, t, :], in0=pa[:], in1=pb_sb[:], op=ALU.mult)
             return prod
@@ -167,15 +168,44 @@ def tile_list_coma_outburst_scores_kernel(
             hq[b, h] = quantise(hb, "h%d%d" % (b, h))
 
         def e_tile(h, t):
-            acc = psum.tile([P, W], F32, name="pa", bufs=4) if h else psum.tile([P, W], F32, name="acc", bufs=2)
+            tag, bufs = [("acc", 3), ("acc", 3), ("acc", 3), ("pa", 3), ("pa", 3), ("pa", 3), ("pb", 2), ("pb", 2)][4 * h + t]
+            acc = psum.tile([P, W], F32, name=tag, bufs=bufs)
             c = slice(P * t, P * (t + 1))
             for b in range(2):
                 nc.tensor.matmul_mx(out=acc[:], lhsT=waq[b][0][:, c].bitcast(FP8X4), lhsT_scale=waq[b][1][:, c],
-                                    rhs=hq[b, h][0][:].bitcast(FP8X4), rhs_scale=hq[b, h][1][:], start=(b == 0), stop=(b == 1))
+                                    rhs=hq[b, h][0][:, :].bitcast(FP8X4), rhs_scale=hq[b, h][1][:, :], start=(b == 0), stop=(b == 1))
             nc.vector.tensor_scalar(out=e[t][:, W * h : W * (h + 1)], in0=acc[:], scalar1=1.0,
                                     scalar2=(top[:, t : t + 1] if h else None), op0=ALU.mult, op1=ALU.max,
                                     accum_out=top[:, 4 * h + t : 4 * h + t + 1])
 
+        qin = keep.tile([P, 12 * W], BF16, name="qin", align_bytes=64)
+
+        def round_into(raw, side, op=nc.scalar.copy):
+            op(out=qin[:, 8 * W * side : 8 * W * side + 4 * W].rearrange("p (u e m j) -> p u m j e", u=2, e=2, j=4),
+                           in_=raw[:].rearrange("p j (m u e) -> p u m j e", u=2, e=2))
+
+        def add_base(b, h, prod, cuts):
+            for eng, j0, j1 in cuts:
+                eng.tensor_tensor(
+                    out=qin[:, 4 * W + 4 * j0 : 4 * W + 4 * j1].rearrange("p (c i t) -> p c t i", i=2, t=4),
+                    in0=prod[:, :, j0:j1].rearrange("p t (c i) -> p c t i", i=2),
+                    in1=base_sb[b, h][:, :, j0:j1].rearrange("p t (c i) -> p c t i", i=2),
+                    op=ALU.add,
+                )
+
+        def quant2(b, h, side):
+            if side is None:
+                hq[b, h] = quantise(qin[:, 4 * W : 8 * W], "h%d%d" % (b, h))
+                return None
+            codes = keep.tile([P, 2 * W], U32, name="hq%d%d_w" % (b, h), align_bytes=64)
+            scales = keep.tile([P, 2 * W], U8, name="hq%d%d_s" % (b, h), align_bytes=64)
+            nc.vector.quantize_mx(out=codes[:].bitcast(FP8X4), scales=scales[:], in_=qin[:, 4 * W * side : 4 * W * side + 8 * W])
+            hq[b, h] = (codes[:, W * (1 - side) : W * (2 - side)], scales[:, W * (1 - side) : W * (2 - side)])
+            return codes[:, W * side : W * (side + 1)], scales[:, W * side : W * (side + 1)]
+
+        GG = [(nc.gpsimd, 0, 256), (nc.gpsimd, 256, W)]
+        G1 = [(nc.gpsimd, 0, W)]
+        VV = [(nc.vector, 0, W)]
         dg = {}
 
         def pick(t, m0, m1):
@@ -186,7 +216,7 @@ def tile_list_coma_outburst_scores_kernel(
             nc.vector.scalar_tensor_tensor(out=yt[:, t, m0:m1], in0=dg[t, g0][:, m0 - g0 : m1 - g0], scalar=dust_sb[:, t : t + 1], in1=yt[:, t, m0:m1],
                                            op0=ALU.add, op1=ALU.mult)
 
-        wbf0 = ring.tile([P, 4 * W], BF16, name="wbf", align_bytes=64)
+        wbf0 = keep.tile([P, 4 * W], BF16, name="wbf", align_bytes=64)
         c0 = keep.tile([P, W], U32, name="w10_w", align_bytes=64)
         s0 = keep.tile([P, W], U8, name="w10_s", align_bytes=64)
         for u in range(2):
@@ -196,30 +226,30 @@ def tile_list_coma_outburst_scores_kernel(
         w1q[0] = (c0, s0)
         gs[1] = stage.tile([P, W], U8, name="gs1", align_bytes=64, offset=0)
         gather_table(1)
-        w1_raw[1] = load_rows(w1[:, W : 2 * W], "w1r1", 0, 512)
+        base_sb[0, 1] = load_base(0, 1, 0, 512)
         base_sb[1, 0] = load_base(1, 0, 1)
         wa_raw[0] = load_rows(wa[0:W, :], "war0", 4)
         wa_raw[1] = load_rows(wa[W : 2 * W, :], "war1", 5)
         prod00 = products(0, 0)
-        prod01 = products(0, 1)
-        finish(0, 0, prod00)
+        add_base(0, 0, prod00, VV)
         base_sb[1, 1] = load_base(1, 1, 2, 512)
-        d_half(0)
-        w1q[1] = quantise(round_weight(w1_raw[1], "s"), "w11")
-        yt = load_rows(obs, "yt", 0, 512)
-        finish(0, 1, prod01)
+        prod01 = products(0, 1)
+        round_into(w1_raw[1], 0)
+        yt = load_rows(obs, "yt", 3)
+        w1q[1] = quant2(0, 0, 0)
+        add_base(0, 1, prod01, VV)
         prod10 = products(1, 0)
-        d_half(1)
-        waq[0] = quantise(round_weight(wa_raw[0], WA_ENG), "wa0")
-        waq[1] = quantise(round_weight(wa_raw[1], WA_ENG), "wa1")
-        finish(1, 0, prod10)
+        round_into(wa_raw[0], 1)
+        waq[0] = quant2(0, 1, 1)
+        add_base(1, 0, prod10, GG)
         prod11 = products(1, 1)
         for t in range(4):
+            d_tile(t)
             pick(t, 0, M)
-            weigh(t, 0, M, 0)
-        for t in range(4):
-            e_tile(0, t)
-        finish(1, 1, prod11)
+        round_into(wa_raw[1], 0)
+        waq[1] = quant2(1, 0, 0)
+        add_base(1, 1, prod11, VV)
+        quant2(1, 1, None)
 
         yb = keep.tile([P, 4 * M], BF16, name="yb", align_bytes=64)
         yw = keep.tile([P, M], U32, name="yw", align_bytes=64)
@@ -227,27 +257,42 @@ def tile_list_coma_outburst_scores_kernel(
         y_rows = out_0.rearrange("(p t) m -> p t m", t=4)
         words_out = out_1[0].rearrange("p m t -> p (m t)").bitcast(I32)
 
+        ntemp = keep.tile([P, 4], F32, name="ntemp")
+        nc.gpsimd.tensor_scalar(out=ntemp[:], in0=temp_sb[:], scalar1=-1.0, scalar2=0.0, op0=ALU.mult, op1=ALU.add)
+        cg = stage.tile([P, 4, M], F32, name="cg", align_bytes=64, offset=9 * R)
+        for t in range(4):
+            nc.scalar.activation(out=cg[:, t, :], in_=dg[t, 0][:], func=ACT.Identity, bias=dust_sb[:, t : t + 1])
+            nc.gpsimd.tensor_tensor(out=yt[:, t, :], in0=cg[:, t, :], in1=yt[:, t, :], op=ALU.mult)
+        a = keep.tile([P, 4, M], F32, name="a")
+
         def look(t, m0, m1):
-            a = ring.tile([P, m1 - m0], F32, name="a", bufs=8)
-            nc.scalar.activation(out=a[:], in_=e[t][:].indirect(p1[:, m0 // 16 : m1 // 16]), func=ACT.Exp,
+            nc.scalar.activation(out=a[:, t, m0:m1], in_=e[t][:].indirect(p1[:, m0 // 16 : m1 // 16]), func=ACT.Exp,
                                  bias=bias[:, t : t + 1], scale=temp_sb[:, t : t + 1])
-            nc.vector.tensor_tensor(out=yt[:, t, m0:m1], in0=yt[:, t, m0:m1], in1=a[:], op=ALU.mult)
 
         def planes(m0, m1):
-            nc.sync.dma_start(out=y_rows[:, :, m0:m1], in_=yt[:, :, m0:m1])
             nc.vector.tensor_copy(out=yb[:, 4 * m0 : 4 * m1].rearrange("p (c i t) -> p c t i", i=2, t=4),
                                   in_=yt[:, :, m0:m1].rearrange("p t (c i) -> p c t i", i=2))
             nc.vector.quantize_mx(out=yw[:, m0:m1].bitcast(FP8X4), scales=ys[:, m0:m1], in_=yb[:, 4 * m0 : 4 * m1])
             nc.sync.dma_start(out=words_out[:, m0:m1], in_=yw[:, m0:m1].bitcast(I32))
 
+        e_tile(0, 0)
         for t in range(4):
+            if t < 3:
+                e_tile(0, t + 1)
             e_tile(1, t)
-            nc.gpsimd.tensor_scalar(out=bias[:, t : t + 1], in0=top[:, 4 + t : 5 + t], scalar1=temp_sb[:, t : t + 1],
-                                    scalar2=-1.0, op0=ALU.mult, op1=ALU.mult)
+            nc.scalar.activation(out=bias[:, t : t + 1], in_=top[:, 4 + t : 5 + t], func=ACT.Copy, scale=ntemp[:, t : t + 1])
+            if t < 3:
+                look(t, 0, M)
+        nc.vector.tensor_tensor(out=yt[:, 0:2, :], in0=yt[:, 0:2, :], in1=a[:, 0:2, :], op=ALU.mult)
+        nc.sync.dma_start(out=y_rows[:, 0:2, :], in_=yt[:, 0:2, :])
+        nc.vector.tensor_tensor(out=yt[:, 2, :], in0=yt[:, 2, :], in1=a[:, 2, :], op=ALU.mult)
+        nc.sync.dma_start(out=y_rows[:, 2, :], in_=yt[:, 2, :])
         for m0 in (0, M // 2):
-            for t in range(4):
-                look(t, m0, m0 + M // 2)
-            planes(m0, m0 + M // 2)
+            m1 = m0 + M // 2
+            look(3, m0, m1)
+            nc.vector.tensor_tensor(out=yt[:, 3, m0:m1], in0=yt[:, 3, m0:m1], in1=a[:, 3, m0:m1], op=ALU.mult)
+            nc.sync.dma_start(out=y_rows[:, 3, m0:m1], in_=yt[:, 3, m0:m1])
+            planes(m0, m1)
         for q in range(4):
             eng = nc.scalar if q % 2 else nc.sync
             eng.dma_start(out=out_2[0, 4 * q : 4 * q + 4, :].bitcast(I32), in_=ys[32 * q : 32 * q + 4, :].bitcast(I32))

@@ -18,9 +18,10 @@ ACT = mybir.ActivationFunctionType
 
 P = 128
 W = 512
-G_ADD = [0,0,0,0]
-WA_ENG = "s"
-CO = "v"
+HW = W // 2
+BIG = 4 * W * 4
+PAD = 512
+SLOT = BIG + PAD
 
 
 def tile_list_coma_outburst_scores_kernel(
@@ -31,268 +32,273 @@ def tile_list_coma_outburst_scores_kernel(
     with ExitStack() as ctx:
         keep = ctx.enter_context(tc.tile_pool(name="keep", bufs=1))
         stage = ctx.enter_context(tc.tile_pool(name="stage", bufs=1))
-        ring = ctx.enter_context(tc.tile_pool(name="ring", bufs=2))
-        psum = ctx.enter_context(tc.psum_pool(name="psum", bufs=2))
+        ring = ctx.enter_context(tc.tile_pool(name="ring", bufs=4))
+        psum = ctx.enter_context(tc.psum_pool(name="psum", bufs=1))
 
-        def scale_rows(engine, plane, rows):
+        def staged(shape, dtype, name, offset):
+            return stage.tile(shape, dtype, name=name, align_bytes=64, offset=offset)
+
+        def kept(shape, dtype, name):
+            return keep.tile(shape, dtype, name=name, align_bytes=64)
+
+        bank_bufs = {"first": 3, "second": 2, "other": 3}
+
+        def bank(tag):
+            return psum.tile([P, W], F32, name=tag, bufs=bank_bufs[tag])
+
+        def load_scale_rows(engine, plane, rows):
             for q in range(4):
-                engine.dma_start(out=plane[32 * q : 32 * q + 4, :].bitcast(I32), in_=rows[0, 4 * q : 4 * q + 4, :].bitcast(I32))
+                engine.dma_start(
+                    out=plane[32 * q : 32 * q + 4, :].bitcast(I32), in_=rows[0, 4 * q : 4 * q + 4, :].bitcast(I32)
+                )
 
-        idx = keep.tile([P, S // 16], U16, name="idx")
-        p1 = keep.tile([P, M // 16], U16, name="p1")
-        p2 = keep.tile([P, M // 16], U16, name="p2")
-        R = 8192 + 512
-        tw = keep.tile([P, T], U32, name="tw", align_bytes=64)
-        ts = stage.tile([P, T], U8, name="ts", align_bytes=64, offset=5 * R - 2048)
-        w2w = stage.tile([P, 2 * H], U8, name="w2w", align_bytes=64, offset=3 * R - 1024)
-        wbw = stage.tile([P, N], U32, name="wbw", align_bytes=64, offset=R - 1024)
-        w2s = stage.tile([P, H], U8, name="w2s", align_bytes=64, offset=6 * R)
-
-        nc.vector.memset(ts[:].bitcast(I32), 0)
-        nc.gpsimd.memset(w2s[:].bitcast(I32), 0)
-
-        nc.sync.dma_start(idx[:], offs)
-        nc.sync.dma_start(p2[:], pos2)
-        nc.sync.dma_start(p1[:], pos1)
-        nc.sync.dma_start(out=wbw[:].bitcast(I32), in_=wb_words[0].rearrange("p n t -> p (n t)").bitcast(I32))
-        nc.sync.dma_start(out=tw[:].bitcast(I32), in_=tab_words[0].rearrange("p n t -> p (n t)").bitcast(I32))
-        nc.sync.dma_start(out=w2w[:].bitcast(I32), in_=w2_words[0].bitcast(I32))
-        scale_rows(nc.sync, ts, tab_scales)
-        scale_rows(nc.gpsimd, w2s, w2_scales)
-
-        def load_rows(rows, name, region, shift=0):
-            raw = stage.tile([P, 4, W], F32, name=name, align_bytes=64, offset=region * R + shift)
+        def load_rows(rows, name, offset):
+            raw = staged([P, 4, W], F32, name, offset)
             nc.sync.dma_start(out=raw[:], in_=rows.rearrange("(p j) c -> p j c", j=4))
             return raw
 
-        def load_base(b, h, region, shift=0):
-            return load_rows(base[W * b : W * (b + 1), W * h : W * (h + 1)], "base%d%d" % (b, h), region, shift)
+        def load_base(b, half, offset):
+            return load_rows(base[W * b : W * (b + 1), W * half : W * (half + 1)], "base%d%d" % (b, half), offset)
 
-        w1_raw = {}
-        wa_raw = {}
+        def mx(out, lhs, lhs_scale, rhs, rhs_scale, start=True, stop=True):
+            nc.tensor.matmul_mx(
+                out=out, lhsT=lhs, lhsT_scale=lhs_scale, rhs=rhs.bitcast(FP8X4), rhs_scale=rhs_scale, start=start, stop=stop
+            )
+
+        idx = keep.tile([P, S // 16], U16, name="idx")
+        gas = keep.tile([P, M // 16], U16, name="gas")
+        cont = keep.tile([P, M // 16], U16, name="cont")
+        tab_w = kept([P, T], U32, "tab_w")
+        tab_s = staged([P, T], U8, "tab_s", 5 * SLOT - T // 2)
+        w2_w = staged([P, 2 * H], U8, "w2_w", 3 * SLOT - H)
+        wb_w = staged([P, N], U32, "wb_w", SLOT - 2 * N)
+        w2_s = staged([P, H], U8, "w2_s", 6 * SLOT)
+
+        nc.vector.memset(tab_s[:].bitcast(I32), 0)
+        nc.gpsimd.memset(w2_s[:].bitcast(I32), 0)
+
+        nc.sync.dma_start(idx[:], offs)
+        nc.sync.dma_start(cont[:], pos2)
+        nc.sync.dma_start(gas[:], pos1)
+        nc.sync.dma_start(out=wb_w[:].bitcast(I32), in_=wb_words[0].rearrange("p n t -> p (n t)").bitcast(I32))
+        nc.sync.dma_start(out=tab_w[:].bitcast(I32), in_=tab_words[0].rearrange("p n t -> p (n t)").bitcast(I32))
+        nc.sync.dma_start(out=w2_w[:].bitcast(I32), in_=w2_words[0].bitcast(I32))
+        load_scale_rows(nc.sync, tab_s, tab_scales)
+        load_scale_rows(nc.gpsimd, w2_s, w2_scales)
+
+        v_w = [kept([P, W], U32, "v_w%d" % half) for half in range(2)]
+        v_s = [kept([P, W], U8, "v_s0")]
+
+        def gather_table(half):
+            entries = idx[:, 32 * half : 32 * (half + 1)]
+            nc.vector.tensor_copy(out=v_w[half][:], in_=tab_w[:].indirect(entries))
+            nc.vector.tensor_copy(out=v_s[half][:], in_=tab_s[:].indirect(entries))
+
+        wb_wd = kept([P, N], U32, "wb_wd")
+        wb_sd = kept([P, N], U8, "wb_sd")
+        w2_wd = kept([P, 2 * H], U8, "w2_wd")
+        w2_sd = kept([P, H], U8, "w2_sd")
         base_sb = {}
 
-        gw = [keep.tile([P, W], U32, name="gw%d" % h, align_bytes=64) for h in range(2)]
-        gs = {0: keep.tile([P, W], U8, name="gs0", align_bytes=64)}
-
-        def gather_table(h):
-            cols = idx[:, 32 * h : 32 * (h + 1)]
-            nc.vector.tensor_copy(out=gw[h][:], in_=tw[:].indirect(cols))
-            nc.vector.tensor_copy(out=gs[h][:], in_=ts[:].indirect(cols))
-
-        wbw_d = keep.tile([P, N], U32, name="wbw_d", align_bytes=64)
-        wbs_d = keep.tile([P, N], U8, name="wbs_d", align_bytes=64)
-        w2w_d = keep.tile([P, 2 * H], U8, name="w2w_d", align_bytes=64)
-        w2s_d = keep.tile([P, H], U8, name="w2s_d", align_bytes=64)
-
-        nc.scalar.copy(out=wbw_d[:].rearrange("p (u e m) -> p u m e", u=2, e=2), in_=wbw[:].rearrange("p (m u e) -> p u m e", u=2, e=2))
-        w1_raw[0] = load_rows(w1[:, 0:W], "w1r0", 0)
-        wbs = stage.tile([P, N], U8, name="wbs", align_bytes=64, offset=R)
-        nc.vector.memset(wbs[:].bitcast(I32), 0)
-        scale_rows(nc.sync, wbs, wb_scales)
-        nc.scalar.copy(out=w2w_d[:].bitcast(U16).rearrange("p (b t m) -> p b t m", b=2, t=4), in_=w2w[:].bitcast(U16).rearrange("p (b m t) -> p b t m", b=2, t=4))
-        base_sb[0, 0] = load_base(0, 0, 2, 512)
-        w1_raw[1] = load_rows(w1[:, W : 2 * W], "w1r1", 3)
+        nc.scalar.copy(
+            out=wb_wd[:].rearrange("p (u e m) -> p u m e", u=2, e=2), in_=wb_w[:].rearrange("p (m u e) -> p u m e", u=2, e=2)
+        )
+        w1_raw0 = load_rows(w1[:, 0:W], "w1_raw0", 0)
+        wb_s = staged([P, N], U8, "wb_s", SLOT)
+        nc.vector.memset(wb_s[:].bitcast(I32), 0)
+        load_scale_rows(nc.sync, wb_s, wb_scales)
+        nc.scalar.copy(
+            out=w2_wd[:].bitcast(U16).rearrange("p (b t m) -> p b t m", b=2, t=4),
+            in_=w2_w[:].bitcast(U16).rearrange("p (b m t) -> p b t m", b=2, t=4),
+        )
+        base_sb[0, 0] = load_base(0, 0, 2 * SLOT + PAD)
+        w1_raw1 = load_rows(w1[:, W:H], "w1_raw1", 3 * SLOT)
         for b in range(2):
-            nc.gpsimd.tensor_copy(out=w2s_d[:, W * b : W * (b + 1)].rearrange("p (t m) -> p t m", t=4), in_=w2s[:, W * b : W * (b + 1)].rearrange("p (m t) -> p t m", t=4))
-        nc.gpsimd.tensor_copy(out=wbs_d[:].rearrange("p (t m) -> p t m", t=4), in_=wbs[:].rearrange("p (m t) -> p t m", t=4))
-        temp_sb = stage.tile([P, 4], F32, name="temp_sb", align_bytes=64, offset=6 * R)
-        dust_sb = stage.tile([P, 4], F32, name="dust_sb", align_bytes=64, offset=6 * R + 64)
+            nc.gpsimd.tensor_copy(
+                out=w2_sd[:, W * b : W * (b + 1)].rearrange("p (t m) -> p t m", t=4),
+                in_=w2_s[:, W * b : W * (b + 1)].rearrange("p (m t) -> p t m", t=4),
+            )
+        nc.gpsimd.tensor_copy(
+            out=wb_sd[:].rearrange("p (t m) -> p t m", t=4), in_=wb_s[:].rearrange("p (m t) -> p t m", t=4)
+        )
+        temp_sb = staged([P, 4], F32, "temp_sb", 6 * SLOT)
+        dust_sb = staged([P, 4], F32, "dust_sb", 6 * SLOT + 64)
         nc.gpsimd.dma_start(out=dust_sb[:], in_=dust.rearrange("(p t) -> p t", t=4))
         nc.gpsimd.dma_start(out=temp_sb[:], in_=temp.rearrange("(p t) -> p t", t=4))
         gather_table(0)
 
-        def round_weight(raw, eng):
-            wbf = ring.tile([P, 4 * W], BF16, name="wbf", align_bytes=64)
-            o = wbf[:].rearrange("p (u e m j) -> p u m j e", u=2, e=2, j=4)
-            i = raw[:].rearrange("p j (m u e) -> p u m j e", u=2, e=2)
-            if eng == "s":
-                nc.scalar.copy(out=o, in_=i)
-            elif eng == "v":
-                nc.vector.tensor_copy(out=o, in_=i)
-            else:
-                nc.gpsimd.tensor_scalar(out=o, in0=i, scalar1=1.0, scalar2=0.0, op0=ALU.mult, op1=ALU.add)
-            return wbf
+        w1_bf = kept([P, 4 * W], BF16, "w1_bf")
+        w1_w0 = kept([P, W], U32, "w1_w0")
+        w1_s0 = kept([P, W], U8, "w1_s0")
+        for u, copy in enumerate((nc.scalar.copy, nc.vector.tensor_copy)):
+            part = w1_bf[:, 2 * W * u : 2 * W * (u + 1)]
+            copy(
+                out=part.rearrange("p (e m j) -> p m j e", e=2, j=4),
+                in_=w1_raw0[:].rearrange("p j (m t) -> p m j t", t=4)[:, :, :, 2 * u : 2 * u + 2],
+            )
+            cols = slice(HW * u, HW * (u + 1))
+            nc.vector.quantize_mx(out=w1_w0[:, cols].bitcast(FP8X4), scales=w1_s0[:, cols], in_=part)
+        w1_q = [(w1_w0, w1_s0)]
+        v_s.append(staged([P, W], U8, "v_s1", 0))
+        gather_table(1)
+        base_sb[0, 1] = load_base(0, 1, PAD)
+        base_sb[1, 0] = load_base(1, 0, SLOT)
+        wa_raw = [load_rows(wa[W * b : W * (b + 1), :], "wa_raw%d" % b, (4 + b) * SLOT) for b in range(2)]
 
-        def quantise(src, name):
-            codes = keep.tile([P, W], U32, name=name + "_w", align_bytes=64)
-            scales = keep.tile([P, W], U8, name=name + "_s", align_bytes=64)
-            nc.vector.quantize_mx(out=codes[:].bitcast(FP8X4), scales=scales[:], in_=src[:, :])
-            return codes, scales
-
-        d = {}
-        e = [keep.tile([P, S], F32, name="e%d" % t) for t in range(4)]
-        top = keep.tile([P, 8], F32, name="top")
-        bias = keep.tile([P, 4], F32, name="bias")
-
-        def d_tile(t):
-            d[t] = stage.tile([P, S], F32, name="d%d" % t, align_bytes=64, offset=[512, 4608, 8 * R, 8 * R + 4096][t])
-            c = slice(P * t, P * (t + 1))
-            for h in range(2):
-                acc = psum.tile([P, W], F32, name="acc", bufs=3)
-                nc.tensor.matmul_mx(out=acc[:], lhsT=wbw_d[:, c].bitcast(FP8X4), lhsT_scale=wbs_d[:, c],
-                                    rhs=gw[h][:].bitcast(FP8X4), rhs_scale=gs[h][:], start=True, stop=True)
-                nc.scalar.copy(out=d[t][:, W * h : W * (h + 1)], in_=acc[:])
-
-        w1q = {}
-        waq = {}
-        hq = {}
-
-        def products(b, h):
-            prod = stage.tile([P, 4, W], F32, name="prod%d%d" % (b, h), align_bytes=64, offset=[7, 8, 7, 9][2 * b + h] * R)
+        def products(b, half, slot, second_tags):
+            prod = staged([P, 4, W], F32, "prod%d%d" % (b, half), slot * SLOT)
+            second = []
+            for t in range(4):
+                c0 = W * b + P * t
+                acc = bank(second_tags[t])
+                mx(acc[:], w2_wd[:, 2 * c0 : 2 * (c0 + P)].bitcast(FP4X4), w2_sd[:, c0 : c0 + P], v_w[half][:], v_s[half][:])
+                held = ring.tile([P, W], F32, name="held")
+                nc.scalar.copy(out=held[:], in_=acc[:])
+                second.append(held)
             for t in range(4):
                 c = slice(P * t, P * (t + 1))
-                g0 = W * b + P * t
-                pb = psum.tile([P, W], F32, name="pb")
-                nc.tensor.matmul_mx(out=pb[:], lhsT=w2w_d[:, 2 * g0 : 2 * (g0 + P)].bitcast(FP4X4), lhsT_scale=w2s_d[:, g0 : g0 + P],
-                                    rhs=gw[h][:].bitcast(FP8X4), rhs_scale=gs[h][:], start=True, stop=True)
-                pa = psum.tile([P, W], F32, name="pa", bufs=3)
-                nc.tensor.matmul_mx(out=pa[:], lhsT=w1q[b][0][:, c].bitcast(FP8X4), lhsT_scale=w1q[b][1][:, c],
-                                    rhs=gw[h][:].bitcast(FP8X4), rhs_scale=gs[h][:], start=True, stop=True)
-                pb_sb = ring.tile([P, W], F32, name="pb_sb", bufs=4)
-                nc.scalar.copy(out=pb_sb[:], in_=pb[:])
-                nc.vector.tensor_tensor(out=prod[:, t, :], in0=pa[:], in1=pb_sb[:], op=ALU.mult)
+                acc = bank("first")
+                mx(acc[:], w1_q[b][0][:, c].bitcast(FP8X4), w1_q[b][1][:, c], v_w[half][:], v_s[half][:])
+                nc.vector.tensor_tensor(out=prod[:, t, :], in0=acc[:], in1=second[t][:], op=ALU.mult)
             return prod
 
-        def finish(b, h, prod):
-            hb = ring.tile([P, 4 * W], BF16, name="hb", align_bytes=64)
-            cut = G_ADD[2 * h + b]
-            for eng, j0, j1 in [(nc.gpsimd, j, j + 128) for j in range(0, cut, 128)] + [(nc.vector, cut, W)]:
-                if j1 > j0:
-                    eng.tensor_tensor(
-                        out=hb[:, 4 * j0 : 4 * j1].rearrange("p (c i t) -> p c t i", i=2, t=4),
-                        in0=prod[:, :, j0:j1].rearrange("p t (c i) -> p c t i", i=2),
-                        in1=base_sb[b, h][:, :, j0:j1].rearrange("p t (c i) -> p c t i", i=2),
-                        op=ALU.add,
-                    )
-            hq[b, h] = quantise(hb, "h%d%d" % (b, h))
+        q_in = kept([P, 12 * W], BF16, "q_in")
+        h_q = {}
 
-        def e_tile(h, t):
-            tag, bufs = [("acc", 3), ("acc", 3), ("acc", 3), ("pa", 3), ("pa", 3), ("pa", 3), ("pb", 2), ("pb", 2)][4 * h + t]
-            acc = psum.tile([P, W], F32, name=tag, bufs=bufs)
-            c = slice(P * t, P * (t + 1))
-            for b in range(2):
-                nc.tensor.matmul_mx(out=acc[:], lhsT=waq[b][0][:, c].bitcast(FP8X4), lhsT_scale=waq[b][1][:, c],
-                                    rhs=hq[b, h][0][:, :].bitcast(FP8X4), rhs_scale=hq[b, h][1][:, :], start=(b == 0), stop=(b == 1))
-            nc.vector.tensor_scalar(out=e[t][:, W * h : W * (h + 1)], in0=acc[:], scalar1=1.0,
-                                    scalar2=(top[:, t : t + 1] if h else None), op0=ALU.mult, op1=ALU.max,
-                                    accum_out=top[:, 4 * h + t : 4 * h + t + 1])
+        def round_weight(raw, side):
+            dst = q_in[:, 8 * W * side : 8 * W * side + 4 * W].rearrange("p (u e m j) -> p u m j e", u=2, e=2, j=4)
+            src = raw[:].rearrange("p j (m u e) -> p u m j e", u=2, e=2)
+            for u in range(2):
+                for m0 in (0, P // 2):
+                    nc.scalar.copy(out=dst[:, u, m0 : m0 + P // 2], in_=src[:, u, m0 : m0 + P // 2])
 
-        qin = keep.tile([P, 12 * W], BF16, name="qin", align_bytes=64)
+        def add_base(engine, b, half, prod, j0, j1):
+            engine.tensor_tensor(
+                out=q_in[:, 4 * W + 4 * j0 : 4 * W + 4 * j1].rearrange("p (c i t) -> p c t i", i=2, t=4),
+                in0=prod[:, :, j0:j1].rearrange("p t (c i) -> p c t i", i=2),
+                in1=base_sb[b, half][:, :, j0:j1].rearrange("p t (c i) -> p c t i", i=2),
+                op=ALU.add,
+            )
 
-        def round_into(raw, side, op=nc.scalar.copy):
-            op(out=qin[:, 8 * W * side : 8 * W * side + 4 * W].rearrange("p (u e m j) -> p u m j e", u=2, e=2, j=4),
-                           in_=raw[:].rearrange("p j (m u e) -> p u m j e", u=2, e=2))
+        def quantise_with_weight(b, half, side):
+            codes = kept([P, 2 * W], U32, "hq%d%d_w" % (b, half))
+            scales = kept([P, 2 * W], U8, "hq%d%d_s" % (b, half))
+            nc.vector.quantize_mx(
+                out=codes[:].bitcast(FP8X4), scales=scales[:], in_=q_in[:, 4 * W * side : 4 * W * side + 8 * W]
+            )
+            unit = slice(W * (1 - side), W * (2 - side))
+            weight = slice(W * side, W * (side + 1))
+            h_q[b, half] = (codes[:, unit], scales[:, unit])
+            return codes[:, weight], scales[:, weight]
 
-        def add_base(b, h, prod, cuts):
-            for eng, j0, j1 in cuts:
-                eng.tensor_tensor(
-                    out=qin[:, 4 * W + 4 * j0 : 4 * W + 4 * j1].rearrange("p (c i t) -> p c t i", i=2, t=4),
-                    in0=prod[:, :, j0:j1].rearrange("p t (c i) -> p c t i", i=2),
-                    in1=base_sb[b, h][:, :, j0:j1].rearrange("p t (c i) -> p c t i", i=2),
-                    op=ALU.add,
-                )
+        steady = ("second",) * 4
+        prod = products(0, 0, 7, ("second", "second", "other", "other"))
+        add_base(nc.vector, 0, 0, prod, 0, W)
+        base_sb[1, 1] = load_base(1, 1, 2 * SLOT + PAD)
+        prod = products(0, 1, 8, steady)
+        round_weight(w1_raw1, 0)
+        weigh = load_rows(obs, "weigh", 3 * SLOT)
+        w1_q.append(quantise_with_weight(0, 0, 0))
+        add_base(nc.vector, 0, 1, prod, 0, W)
+        prod = products(1, 0, 7, steady)
+        round_weight(wa_raw[0], 1)
+        wa_q = [quantise_with_weight(0, 1, 1)]
 
-        def quant2(b, h, side):
-            if side is None:
-                hq[b, h] = quantise(qin[:, 4 * W : 8 * W], "h%d%d" % (b, h))
-                return None
-            codes = keep.tile([P, 2 * W], U32, name="hq%d%d_w" % (b, h), align_bytes=64)
-            scales = keep.tile([P, 2 * W], U8, name="hq%d%d_s" % (b, h), align_bytes=64)
-            nc.vector.quantize_mx(out=codes[:].bitcast(FP8X4), scales=scales[:], in_=qin[:, 4 * W * side : 4 * W * side + 8 * W])
-            hq[b, h] = (codes[:, W * (1 - side) : W * (2 - side)], scales[:, W * (1 - side) : W * (2 - side)])
-            return codes[:, W * side : W * (side + 1)], scales[:, W * side : W * (side + 1)]
-
-        GG = [(nc.gpsimd, 0, 256), (nc.gpsimd, 256, W)]
-        G1 = [(nc.gpsimd, 0, W)]
-        VV = [(nc.vector, 0, W)]
-        dg = {}
-
-        def pick(t, m0, m1):
-            dg[t, m0] = keep.tile([P, m1 - m0], F32, name="dg%d_%d" % (t, m0))
-            nc.vector.tensor_copy(out=dg[t, m0][:], in_=d[t][:].indirect(p2[:, m0 // 16 : m1 // 16]))
-
-        def weigh(t, m0, m1, g0):
-            nc.vector.scalar_tensor_tensor(out=yt[:, t, m0:m1], in0=dg[t, g0][:, m0 - g0 : m1 - g0], scalar=dust_sb[:, t : t + 1], in1=yt[:, t, m0:m1],
-                                           op0=ALU.add, op1=ALU.mult)
-
-        wbf0 = keep.tile([P, 4 * W], BF16, name="wbf", align_bytes=64)
-        c0 = keep.tile([P, W], U32, name="w10_w", align_bytes=64)
-        s0 = keep.tile([P, W], U8, name="w10_s", align_bytes=64)
-        for u in range(2):
-            (nc.vector.tensor_copy if u else nc.scalar.copy)(out=wbf0[:, 2 * W * u : 2 * W * (u + 1)].rearrange("p (t m j) -> p m j t", t=2, j=4),
-                           in_=w1_raw[0][:].rearrange("p j (m t) -> p m j t", t=4)[:, :, :, 2 * u : 2 * u + 2])
-            nc.vector.quantize_mx(out=c0[:, 256 * u : 256 * (u + 1)].bitcast(FP8X4), scales=s0[:, 256 * u : 256 * (u + 1)], in_=wbf0[:, 2 * W * u : 2 * W * (u + 1)])
-        w1q[0] = (c0, s0)
-        gs[1] = stage.tile([P, W], U8, name="gs1", align_bytes=64, offset=0)
-        gather_table(1)
-        base_sb[0, 1] = load_base(0, 1, 0, 512)
-        base_sb[1, 0] = load_base(1, 0, 1)
-        wa_raw[0] = load_rows(wa[0:W, :], "war0", 4)
-        wa_raw[1] = load_rows(wa[W : 2 * W, :], "war1", 5)
-        prod00 = products(0, 0)
-        add_base(0, 0, prod00, VV)
-        base_sb[1, 1] = load_base(1, 1, 2, 512)
-        prod01 = products(0, 1)
-        round_into(w1_raw[1], 0)
-        yt = load_rows(obs, "yt", 3)
-        w1q[1] = quant2(0, 0, 0)
-        add_base(0, 1, prod01, VV)
-        prod10 = products(1, 0)
-        round_into(wa_raw[0], 1)
-        waq[0] = quant2(0, 1, 1)
-        add_base(1, 0, prod10, GG)
-        prod11 = products(1, 1)
+        for j0 in (0, HW):
+            add_base(nc.gpsimd, 1, 0, prod, j0, j0 + HW)
+        prod = products(1, 1, 9, steady)
+        picked = []
         for t in range(4):
-            d_tile(t)
-            pick(t, 0, M)
-        round_into(wa_raw[1], 0)
-        waq[1] = quant2(1, 0, 0)
-        add_base(1, 1, prod11, VV)
-        quant2(1, 1, None)
+            d = staged([P, S], F32, "d%d" % t, (PAD if t < 2 else 8 * SLOT) + (t % 2) * 4 * S)
+            c = slice(P * t, P * (t + 1))
+            for half in range(2):
+                acc = bank("other")
+                mx(acc[:], wb_wd[:, c].bitcast(FP8X4), wb_sd[:, c], v_w[half][:], v_s[half][:])
+                nc.scalar.copy(out=d[:, W * half : W * (half + 1)], in_=acc[:])
+            pick = keep.tile([P, M], F32, name="pick%d" % t)
+            nc.vector.tensor_copy(out=pick[:], in_=d[:].indirect(cont[:]))
+            picked.append(pick)
+        round_weight(wa_raw[1], 0)
+        wa_q.append(quantise_with_weight(1, 0, 0))
 
-        yb = keep.tile([P, 4 * M], BF16, name="yb", align_bytes=64)
-        yw = keep.tile([P, M], U32, name="yw", align_bytes=64)
-        ys = keep.tile([P, M], U8, name="ys", align_bytes=64)
+        for j0 in (0, HW):
+            add_base(nc.vector, 1, 1, prod, j0, j0 + HW)
+        last_w = kept([P, W], U32, "last_w")
+        last_s = kept([P, W], U8, "last_s")
+        for j0 in (0, HW):
+            nc.vector.quantize_mx(
+                out=last_w[:, j0 : j0 + HW].bitcast(FP8X4),
+                scales=last_s[:, j0 : j0 + HW],
+                in_=q_in[:, 4 * W + 4 * j0 : 4 * W + 4 * (j0 + HW)],
+            )
+        h_q[1, 1] = (last_w, last_s)
+
+        top = staged([P, 8], F32, "top", 7 * SLOT)
+        offset_d = staged([P, 4, M], F32, "offset_d", 9 * SLOT)
+        for t in range(4):
+            nc.scalar.activation(out=offset_d[:, t, :], in_=picked[t][:], func=ACT.Identity, bias=dust_sb[:, t : t + 1])
+            nc.gpsimd.tensor_tensor(out=weigh[:, t, :], in0=offset_d[:, t, :], in1=weigh[:, t, :], op=ALU.mult)
+
+        e = [keep.tile([P, S], F32, name="e%d" % t) for t in range(4)]
+        bias = keep.tile([P, 4], F32, name="bias")
+        a = keep.tile([P, 4, M], F32, name="a")
+        e_tags = [tag for tag in ("other", "first", "second") for n in range(bank_bufs[tag])]
+
+        def e_half(half, t):
+            acc = bank(e_tags[4 * half + t])
+            c = slice(P * t, P * (t + 1))
+            passes = [(0, 0, W), (1, 0, HW), (1, HW, W)] if half else [(0, 0, W), (1, 0, W)]
+            for b, j0, j1 in passes:
+                codes, scales = h_q[b, half]
+                mx(acc[:, j0:j1], wa_q[b][0][:, c].bitcast(FP8X4), wa_q[b][1][:, c], codes[:, j0:j1], scales[:, j0:j1],
+                   start=(b == 0), stop=(b == 1 and j1 == W))
+            nc.vector.tensor_scalar(
+                out=e[t][:, W * half : W * (half + 1)], in0=acc[:], scalar1=1.0,
+                scalar2=(top[:, t : t + 1] if half else None), op0=ALU.mult, op1=ALU.max,
+                accum_out=top[:, 4 * half + t : 4 * half + t + 1],
+            )
+
+        def look(t, m0, m1):
+            nc.scalar.activation(
+                out=a[:, t, m0:m1], in_=e[t][:].indirect(gas[:, m0 // 16 : m1 // 16]), func=ACT.Exp,
+                bias=bias[:, t : t + 1], scale=temp_sb[:, t : t + 1],
+            )
+
+        e_half(0, 0)
+        for t in range(4):
+            if t < 3:
+                e_half(0, t + 1)
+            e_half(1, t)
+            nc.vector.tensor_scalar(
+                out=bias[:, t : t + 1], in0=top[:, 4 + t : 5 + t], scalar1=temp_sb[:, t : t + 1], scalar2=-1.0,
+                op0=ALU.mult, op1=ALU.mult,
+            )
+            if t < 3:
+                look(t, 0, M)
+
+        y = staged([P, 4, M], F32, "y", 7 * SLOT)
+        y_bf = kept([P, 4 * M], BF16, "y_bf")
+        y_w = kept([P, M], U32, "y_w")
+        y_s = kept([P, M], U8, "y_s")
         y_rows = out_0.rearrange("(p t) m -> p t m", t=4)
         words_out = out_1[0].rearrange("p m t -> p (m t)").bitcast(I32)
 
-        ntemp = keep.tile([P, 4], F32, name="ntemp")
-        nc.gpsimd.tensor_scalar(out=ntemp[:], in0=temp_sb[:], scalar1=-1.0, scalar2=0.0, op0=ALU.mult, op1=ALU.add)
-        cg = stage.tile([P, 4, M], F32, name="cg", align_bytes=64, offset=9 * R)
-        for t in range(4):
-            nc.scalar.activation(out=cg[:, t, :], in_=dg[t, 0][:], func=ACT.Identity, bias=dust_sb[:, t : t + 1])
-            nc.gpsimd.tensor_tensor(out=yt[:, t, :], in0=cg[:, t, :], in1=yt[:, t, :], op=ALU.mult)
-        a = keep.tile([P, 4, M], F32, name="a")
+        def finish_y(t0, t1, m0, m1):
+            nc.vector.tensor_tensor(out=y[:, t0:t1, m0:m1], in0=weigh[:, t0:t1, m0:m1], in1=a[:, t0:t1, m0:m1], op=ALU.mult)
+            nc.sync.dma_start(out=y_rows[:, t0:t1, m0:m1], in_=y[:, t0:t1, m0:m1])
 
-        def look(t, m0, m1):
-            nc.scalar.activation(out=a[:, t, m0:m1], in_=e[t][:].indirect(p1[:, m0 // 16 : m1 // 16]), func=ACT.Exp,
-                                 bias=bias[:, t : t + 1], scale=temp_sb[:, t : t + 1])
-
-        def planes(m0, m1):
-            nc.vector.tensor_copy(out=yb[:, 4 * m0 : 4 * m1].rearrange("p (c i t) -> p c t i", i=2, t=4),
-                                  in_=yt[:, :, m0:m1].rearrange("p t (c i) -> p c t i", i=2))
-            nc.vector.quantize_mx(out=yw[:, m0:m1].bitcast(FP8X4), scales=ys[:, m0:m1], in_=yb[:, 4 * m0 : 4 * m1])
-            nc.sync.dma_start(out=words_out[:, m0:m1], in_=yw[:, m0:m1].bitcast(I32))
-
-        e_tile(0, 0)
-        for t in range(4):
-            if t < 3:
-                e_tile(0, t + 1)
-            e_tile(1, t)
-            nc.scalar.activation(out=bias[:, t : t + 1], in_=top[:, 4 + t : 5 + t], func=ACT.Copy, scale=ntemp[:, t : t + 1])
-            if t < 3:
-                look(t, 0, M)
-        nc.vector.tensor_tensor(out=yt[:, 0:2, :], in0=yt[:, 0:2, :], in1=a[:, 0:2, :], op=ALU.mult)
-        nc.sync.dma_start(out=y_rows[:, 0:2, :], in_=yt[:, 0:2, :])
-        nc.vector.tensor_tensor(out=yt[:, 2, :], in0=yt[:, 2, :], in1=a[:, 2, :], op=ALU.mult)
-        nc.sync.dma_start(out=y_rows[:, 2, :], in_=yt[:, 2, :])
+        finish_y(0, 2, 0, M)
+        finish_y(2, 3, 0, M)
         for m0 in (0, M // 2):
             m1 = m0 + M // 2
             look(3, m0, m1)
-            nc.vector.tensor_tensor(out=yt[:, 3, m0:m1], in0=yt[:, 3, m0:m1], in1=a[:, 3, m0:m1], op=ALU.mult)
-            nc.sync.dma_start(out=y_rows[:, 3, m0:m1], in_=yt[:, 3, m0:m1])
-            planes(m0, m1)
+            finish_y(3, 4, m0, m1)
+            nc.vector.tensor_copy(
+                out=y_bf[:, 4 * m0 : 4 * m1].rearrange("p (c i t) -> p c t i", i=2, t=4),
+                in_=y[:, :, m0:m1].rearrange("p t (c i) -> p c t i", i=2),
+            )
+            nc.vector.quantize_mx(out=y_w[:, m0:m1].bitcast(FP8X4), scales=y_s[:, m0:m1], in_=y_bf[:, 4 * m0 : 4 * m1])
+            nc.sync.dma_start(out=words_out[:, m0:m1], in_=y_w[:, m0:m1].bitcast(I32))
         for q in range(4):
-            eng = nc.scalar if q % 2 else nc.sync
-            eng.dma_start(out=out_2[0, 4 * q : 4 * q + 4, :].bitcast(I32), in_=ys[32 * q : 32 * q + 4, :].bitcast(I32))
+            engine = nc.scalar if q % 2 else nc.sync
+            engine.dma_start(out=out_2[0, 4 * q : 4 * q + 4, :].bitcast(I32), in_=y_s[32 * q : 32 * q + 4, :].bitcast(I32))

@@ -19,6 +19,7 @@ ACT = mybir.ActivationFunctionType
 P = 128
 W = 512
 HW = W // 2
+ALIGN = 64
 BIG = 4 * W * 4
 PAD = 512
 SLOT = BIG + PAD
@@ -36,10 +37,10 @@ def tile_list_coma_outburst_scores_kernel(
         psum = ctx.enter_context(tc.psum_pool(name="psum", bufs=1))
 
         def staged(shape, dtype, name, offset):
-            return stage.tile(shape, dtype, name=name, align_bytes=64, offset=offset)
+            return stage.tile(shape, dtype, name=name, align_bytes=ALIGN, offset=offset)
 
         def kept(shape, dtype, name):
-            return keep.tile(shape, dtype, name=name, align_bytes=64)
+            return keep.tile(shape, dtype, name=name, align_bytes=ALIGN)
 
         bank_bufs = {"first": 3, "second": 2, "other": 3}
 
@@ -90,7 +91,7 @@ def tile_list_coma_outburst_scores_kernel(
         v_s = [kept([P, W], U8, "v_s0")]
 
         def gather_table(half):
-            entries = idx[:, 32 * half : 32 * (half + 1)]
+            entries = idx[:, W // 16 * half : W // 16 * (half + 1)]
             nc.vector.tensor_copy(out=v_w[half][:], in_=tab_w[:].indirect(entries))
             nc.vector.tensor_copy(out=v_s[half][:], in_=tab_s[:].indirect(entries))
 
@@ -122,7 +123,7 @@ def tile_list_coma_outburst_scores_kernel(
             out=wb_sd[:].rearrange("p (t m) -> p t m", t=4), in_=wb_s[:].rearrange("p (m t) -> p t m", t=4)
         )
         temp_sb = staged([P, 4], F32, "temp_sb", 6 * SLOT)
-        dust_sb = staged([P, 4], F32, "dust_sb", 6 * SLOT + 64)
+        dust_sb = staged([P, 4], F32, "dust_sb", 6 * SLOT + ALIGN)
         nc.gpsimd.dma_start(out=dust_sb[:], in_=dust.rearrange("(p t) -> p t", t=4))
         nc.gpsimd.dma_start(out=temp_sb[:], in_=temp.rearrange("(p t) -> p t", t=4))
         gather_table(0)
@@ -142,8 +143,8 @@ def tile_list_coma_outburst_scores_kernel(
         v_s.append(staged([P, W], U8, "v_s1", 0))
         gather_table(1)
         base_sb[0, 1] = load_base(0, 1, PAD)
-        base_sb[1, 0] = load_base(1, 0, SLOT)
-        wa_raw = [load_rows(wa[W * b : W * (b + 1), :], "wa_raw%d" % b, (4 + b) * SLOT) for b in range(2)]
+        wa_raw = [load_rows(wa[W * b : W * (b + 1), :], "wa_raw%d" % b, (1, 4)[b] * SLOT) for b in range(2)]
+        base_sb[1, 0] = load_base(1, 0, 5 * SLOT)
 
         def products(b, half, slot, second_tags):
             prod = staged([P, 4, W], F32, "prod%d%d" % (b, half), slot * SLOT)
@@ -195,13 +196,13 @@ def tile_list_coma_outburst_scores_kernel(
         prod = products(0, 0, 7, ("second", "second", "other", "other"))
         add_base(nc.vector, 0, 0, prod, 0, W)
         base_sb[1, 1] = load_base(1, 1, 2 * SLOT + PAD)
-        prod = products(0, 1, 8, steady)
         round_weight(w1_raw1, 0)
-        weigh = load_rows(obs, "weigh", 3 * SLOT)
+        factor = load_rows(obs, "factor", 3 * SLOT)
+        prod = products(0, 1, 8, steady)
         w1_q.append(quantise_with_weight(0, 0, 0))
         add_base(nc.vector, 0, 1, prod, 0, W)
-        prod = products(1, 0, 7, steady)
         round_weight(wa_raw[0], 1)
+        prod = products(1, 0, 7, steady)
         wa_q = [quantise_with_weight(0, 1, 1)]
 
         for j0 in (0, HW):
@@ -237,12 +238,12 @@ def tile_list_coma_outburst_scores_kernel(
         offset_d = staged([P, 4, M], F32, "offset_d", 9 * SLOT)
         for t in range(4):
             nc.scalar.activation(out=offset_d[:, t, :], in_=picked[t][:], func=ACT.Identity, bias=dust_sb[:, t : t + 1])
-            nc.gpsimd.tensor_tensor(out=weigh[:, t, :], in0=offset_d[:, t, :], in1=weigh[:, t, :], op=ALU.mult)
+            nc.gpsimd.tensor_tensor(out=factor[:, t, :], in0=offset_d[:, t, :], in1=factor[:, t, :], op=ALU.mult)
 
         e = [keep.tile([P, S], F32, name="e%d" % t) for t in range(4)]
         bias = keep.tile([P, 4], F32, name="bias")
         a = keep.tile([P, 4, M], F32, name="a")
-        e_tags = [tag for tag in ("other", "first", "second") for n in range(bank_bufs[tag])]
+        e_tags = sum(([tag] * bank_bufs[tag] for tag in ("other", "first", "second")), [])
 
         def e_half(half, t):
             acc = bank(e_tags[4 * half + t])
@@ -284,7 +285,7 @@ def tile_list_coma_outburst_scores_kernel(
         words_out = out_1[0].rearrange("p m t -> p (m t)").bitcast(I32)
 
         def finish_y(t0, t1, m0, m1):
-            nc.vector.tensor_tensor(out=y[:, t0:t1, m0:m1], in0=weigh[:, t0:t1, m0:m1], in1=a[:, t0:t1, m0:m1], op=ALU.mult)
+            nc.vector.tensor_tensor(out=y[:, t0:t1, m0:m1], in0=factor[:, t0:t1, m0:m1], in1=a[:, t0:t1, m0:m1], op=ALU.mult)
             nc.sync.dma_start(out=y_rows[:, t0:t1, m0:m1], in_=y[:, t0:t1, m0:m1])
 
         finish_y(0, 2, 0, M)

from contextlib import ExitStack

import concourse.mybir as mybir

K, H, N, T, S, M = 512, 1024, 512, 4096, 1024, 512
FLOPS = 2 * (2 * K * H * S + H * N * S + K * N * S)

F32 = mybir.dt.float32
BF16 = mybir.dt.bfloat16
I32 = mybir.dt.int32
U32 = mybir.dt.uint32
U16 = mybir.dt.uint16
U8 = mybir.dt.uint8
FP8X4 = mybir.dt.float8_e4m3fn_x4
FP4X4 = mybir.dt.float4_e2m1fn_x4
ALU = mybir.AluOpType
ACT = mybir.ActivationFunctionType

P = 128
W = 512
HW = W // 2
ALIGN = 64
BIG = 4 * W * 4
PAD = 512
SLOT = BIG + PAD


def tile_list_coma_outburst_scores_kernel(
    tc, tab_words, tab_scales, offs, pos1, pos2, w1, w2_words, w2_scales, base, wa,
    wb_words, wb_scales, temp, dust, obs, out_0, out_1, out_2,
):
    nc = tc.nc
    with ExitStack() as ctx:
        keep = ctx.enter_context(tc.tile_pool(name="keep", bufs=1))
        stage = ctx.enter_context(tc.tile_pool(name="stage", bufs=1))
        ring = ctx.enter_context(tc.tile_pool(name="ring", bufs=4))
        psum = ctx.enter_context(tc.psum_pool(name="psum", bufs=1))

        def staged(shape, dtype, name, offset):
            return stage.tile(shape, dtype, name=name, align_bytes=ALIGN, offset=offset)

        def kept(shape, dtype, name):
            return keep.tile(shape, dtype, name=name, align_bytes=ALIGN)

        bank_bufs = {"first": 3, "second": 2, "other": 3}

        def bank(tag):
            return psum.tile([P, W], F32, name=tag, bufs=bank_bufs[tag])

        def load_scale_rows(engine, plane, rows):
            for q in range(4):
                engine.dma_start(
                    out=plane[32 * q : 32 * q + 4, :].bitcast(I32), in_=rows[0, 4 * q : 4 * q + 4, :].bitcast(I32)
                )

        def load_rows(rows, name, offset):
            raw = staged([P, 4, W], F32, name, offset)
            nc.sync.dma_start(out=raw[:], in_=rows.rearrange("(p j) c -> p j c", j=4))
            return raw

        def load_base(b, half, offset):
            return load_rows(base[W * b : W * (b + 1), W * half : W * (half + 1)], "base%d%d" % (b, half), offset)

        def mx(out, lhs, lhs_scale, rhs, rhs_scale, start=True, stop=True):
            nc.tensor.matmul_mx(
                out=out, lhsT=lhs, lhsT_scale=lhs_scale, rhs=rhs.bitcast(FP8X4), rhs_scale=rhs_scale, start=start, stop=stop
            )

        idx = keep.tile([P, S // 16], U16, name="idx")
        gas = keep.tile([P, M // 16], U16, name="gas")
        cont = keep.tile([P, M // 16], U16, name="cont")
        tab_w = kept([P, T], U32, "tab_w")
        tab_s = staged([P, T], U8, "tab_s", 5 * SLOT - T // 2)
        w2_w = staged([P, 2 * H], U8, "w2_w", 3 * SLOT - H)
        wb_w = staged([P, N], U32, "wb_w", SLOT - 2 * N)
        w2_s = staged([P, H], U8, "w2_s", 6 * SLOT)

        nc.vector.memset(tab_s[:].bitcast(I32), 0)
        nc.gpsimd.memset(w2_s[:].bitcast(I32), 0)

        nc.sync.dma_start(idx[:], offs)
        nc.sync.dma_start(cont[:], pos2)
        nc.sync.dma_start(gas[:], pos1)
        nc.sync.dma_start(out=wb_w[:].bitcast(I32), in_=wb_words[0].rearrange("p n t -> p (n t)").bitcast(I32))
        nc.sync.dma_start(out=tab_w[:].bitcast(I32), in_=tab_words[0].rearrange("p n t -> p (n t)").bitcast(I32))
        nc.sync.dma_start(out=w2_w[:].bitcast(I32), in_=w2_words[0].bitcast(I32))
        load_scale_rows(nc.sync, tab_s, tab_scales)
        load_scale_rows(nc.gpsimd, w2_s, w2_scales)

        v_w = [kept([P, W], U32, "v_w%d" % half) for half in range(2)]
        v_s = [kept([P, W], U8, "v_s0")]

        def gather_table(half):
            entries = idx[:, W // 16 * half : W // 16 * (half + 1)]
            nc.vector.tensor_copy(out=v_w[half][:], in_=tab_w[:].indirect(entries))
            nc.vector.tensor_copy(out=v_s[half][:], in_=tab_s[:].indirect(entries))

        wb_wd = kept([P, N], U32, "wb_wd")
        wb_sd = kept([P, N], U8, "wb_sd")
        w2_wd = kept([P, 2 * H], U8, "w2_wd")
        w2_sd = kept([P, H], U8, "w2_sd")
        base_sb = {}

        nc.scalar.copy(
            out=wb_wd[:].rearrange("p (u e m) -> p u m e", u=2, e=2), in_=wb_w[:].rearrange("p (m u e) -> p u m e", u=2, e=2)
        )
        w1_raw0 = load_rows(w1[:, 0:W], "w1_raw0", 0)
        wb_s = staged([P, N], U8, "wb_s", SLOT)
        nc.vector.memset(wb_s[:].bitcast(I32), 0)
        load_scale_rows(nc.sync, wb_s, wb_scales)
        nc.scalar.copy(
            out=w2_wd[:].bitcast(U16).rearrange("p (b t m) -> p b t m", b=2, t=4),
            in_=w2_w[:].bitcast(U16).rearrange("p (b m t) -> p b t m", b=2, t=4),
        )
        base_sb[0, 0] = load_base(0, 0, 2 * SLOT + PAD)
        w1_raw1 = load_rows(w1[:, W:H], "w1_raw1", 3 * SLOT)
        for b in range(2):
            nc.gpsimd.tensor_copy(
                out=w2_sd[:, W * b : W * (b + 1)].rearrange("p (t m) -> p t m", t=4),
                in_=w2_s[:, W * b : W * (b + 1)].rearrange("p (m t) -> p t m", t=4),
            )
        nc.gpsimd.tensor_copy(
            out=wb_sd[:].rearrange("p (t m) -> p t m", t=4), in_=wb_s[:].rearrange("p (m t) -> p t m", t=4)
        )
        temp_sb = staged([P, 4], F32, "temp_sb", 6 * SLOT)
        dust_sb = staged([P, 4], F32, "dust_sb", 6 * SLOT + ALIGN)
        nc.gpsimd.dma_start(out=dust_sb[:], in_=dust.rearrange("(p t) -> p t", t=4))
        nc.gpsimd.dma_start(out=temp_sb[:], in_=temp.rearrange("(p t) -> p t", t=4))
        gather_table(0)

        w1_bf = kept([P, 4 * W], BF16, "w1_bf")
        w1_w0 = kept([P, W], U32, "w1_w0")
        w1_s0 = kept([P, W], U8, "w1_s0")
        for u, copy in enumerate((nc.scalar.copy, nc.vector.tensor_copy)):
            part = w1_bf[:, 2 * W * u : 2 * W * (u + 1)]
            copy(
                out=part.rearrange("p (e m j) -> p m j e", e=2, j=4),
                in_=w1_raw0[:].rearrange("p j (m t) -> p m j t", t=4)[:, :, :, 2 * u : 2 * u + 2],
            )
            cols = slice(HW * u, HW * (u + 1))
            nc.vector.quantize_mx(out=w1_w0[:, cols].bitcast(FP8X4), scales=w1_s0[:, cols], in_=part)
        w1_q = [(w1_w0, w1_s0)]
        v_s.append(staged([P, W], U8, "v_s1", 0))
        gather_table(1)
        base_sb[0, 1] = load_base(0, 1, PAD)
        wa_raw = [load_rows(wa[W * b : W * (b + 1), :], "wa_raw%d" % b, (1, 4)[b] * SLOT) for b in range(2)]
        base_sb[1, 0] = load_base(1, 0, 5 * SLOT)

        def products(b, half, slot, second_tags):
            prod = staged([P, 4, W], F32, "prod%d%d" % (b, half), slot * SLOT)
            second = []
            for t in range(4):
                c0 = W * b + P * t
                acc = bank(second_tags[t])
                mx(acc[:], w2_wd[:, 2 * c0 : 2 * (c0 + P)].bitcast(FP4X4), w2_sd[:, c0 : c0 + P], v_w[half][:], v_s[half][:])
                held = ring.tile([P, W], F32, name="held")
                nc.scalar.copy(out=held[:], in_=acc[:])
                second.append(held)
            for t in range(4):
                c = slice(P * t, P * (t + 1))
                acc = bank("first")
                mx(acc[:], w1_q[b][0][:, c].bitcast(FP8X4), w1_q[b][1][:, c], v_w[half][:], v_s[half][:])
                nc.vector.tensor_tensor(out=prod[:, t, :], in0=acc[:], in1=second[t][:], op=ALU.mult)
            return prod

        q_in = kept([P, 12 * W], BF16, "q_in")
        h_q = {}

        def round_weight(raw, side):
            dst = q_in[:, 8 * W * side : 8 * W * side + 4 * W].rearrange("p (u e m j) -> p u m j e", u=2, e=2, j=4)
            src = raw[:].rearrange("p j (m u e) -> p u m j e", u=2, e=2)
            for u in range(2):
                for m0 in (0, P // 2):
                    nc.scalar.copy(out=dst[:, u, m0 : m0 + P // 2], in_=src[:, u, m0 : m0 + P // 2])

        def add_base(engine, b, half, prod, j0, j1):
            engine.tensor_tensor(
                out=q_in[:, 4 * W + 4 * j0 : 4 * W + 4 * j1].rearrange("p (c i t) -> p c t i", i=2, t=4),
                in0=prod[:, :, j0:j1].rearrange("p t (c i) -> p c t i", i=2),
                in1=base_sb[b, half][:, :, j0:j1].rearrange("p t (c i) -> p c t i", i=2),
                op=ALU.add,
            )

        def quantise_with_weight(b, half, side):
            codes = kept([P, 2 * W], U32, "hq%d%d_w" % (b, half))
            scales = kept([P, 2 * W], U8, "hq%d%d_s" % (b, half))
            nc.vector.quantize_mx(
                out=codes[:].bitcast(FP8X4), scales=scales[:], in_=q_in[:, 4 * W * side : 4 * W * side + 8 * W]
            )
            unit = slice(W * (1 - side), W * (2 - side))
            weight = slice(W * side, W * (side + 1))
            h_q[b, half] = (codes[:, unit], scales[:, unit])
            return codes[:, weight], scales[:, weight]

        steady = ("second",) * 4
        prod = products(0, 0, 7, ("second", "second", "other", "other"))
        add_base(nc.vector, 0, 0, prod, 0, W)
        base_sb[1, 1] = load_base(1, 1, 2 * SLOT + PAD)
        round_weight(w1_raw1, 0)
        factor = load_rows(obs, "factor", 3 * SLOT)
        prod = products(0, 1, 8, steady)
        w1_q.append(quantise_with_weight(0, 0, 0))
        add_base(nc.vector, 0, 1, prod, 0, W)
        round_weight(wa_raw[0], 1)
        prod = products(1, 0, 7, steady)
        wa_q = [quantise_with_weight(0, 1, 1)]

        for j0 in (0, HW):
            add_base(nc.gpsimd, 1, 0, prod, j0, j0 + HW)
        prod = products(1, 1, 9, steady)
        picked = []
        for t in range(4):
            d = staged([P, S], F32, "d%d" % t, (PAD if t < 2 else 8 * SLOT) + (t % 2) * 4 * S)
            c = slice(P * t, P * (t + 1))
            for half in range(2):
                acc = bank("other")
                mx(acc[:], wb_wd[:, c].bitcast(FP8X4), wb_sd[:, c], v_w[half][:], v_s[half][:])
                nc.scalar.copy(out=d[:, W * half : W * (half + 1)], in_=acc[:])
            pick = keep.tile([P, M], F32, name="pick%d" % t)
            nc.vector.tensor_copy(out=pick[:], in_=d[:].indirect(cont[:]))
            picked.append(pick)
        round_weight(wa_raw[1], 0)
        wa_q.append(quantise_with_weight(1, 0, 0))

        for j0 in (0, HW):
            add_base(nc.vector, 1, 1, prod, j0, j0 + HW)
        last_w = kept([P, W], U32, "last_w")
        last_s = kept([P, W], U8, "last_s")
        for j0 in (0, HW):
            nc.vector.quantize_mx(
                out=last_w[:, j0 : j0 + HW].bitcast(FP8X4),
                scales=last_s[:, j0 : j0 + HW],
                in_=q_in[:, 4 * W + 4 * j0 : 4 * W + 4 * (j0 + HW)],
            )
        h_q[1, 1] = (last_w, last_s)

        top = staged([P, 8], F32, "top", 7 * SLOT)
        offset_d = staged([P, 4, M], F32, "offset_d", 9 * SLOT)
        for t in range(4):
            nc.scalar.activation(out=offset_d[:, t, :], in_=picked[t][:], func=ACT.Identity, bias=dust_sb[:, t : t + 1])
            nc.gpsimd.tensor_tensor(out=factor[:, t, :], in0=offset_d[:, t, :], in1=factor[:, t, :], op=ALU.mult)

        e = [keep.tile([P, S], F32, name="e%d" % t) for t in range(4)]
        bias = keep.tile([P, 4], F32, name="bias")
        a = keep.tile([P, 4, M], F32, name="a")
        e_tags = sum(([tag] * bank_bufs[tag] for tag in ("other", "first", "second")), [])

        def e_half(half, t):
            acc = bank(e_tags[4 * half + t])
            c = slice(P * t, P * (t + 1))
            passes = [(0, 0, W), (1, 0, HW), (1, HW, W)] if half else [(0, 0, W), (1, 0, W)]
            for b, j0, j1 in passes:
                codes, scales = h_q[b, half]
                mx(acc[:, j0:j1], wa_q[b][0][:, c].bitcast(FP8X4), wa_q[b][1][:, c], codes[:, j0:j1], scales[:, j0:j1],
                   start=(b == 0), stop=(b == 1 and j1 == W))
            nc.vector.tensor_scalar(
                out=e[t][:, W * half : W * (half + 1)], in0=acc[:], scalar1=1.0,
                scalar2=(top[:, t : t + 1] if half else None), op0=ALU.mult, op1=ALU.max,
                accum_out=top[:, 4 * half + t : 4 * half + t + 1],
            )

        def look(t, m0, m1):
            nc.scalar.activation(
                out=a[:, t, m0:m1], in_=e[t][:].indirect(gas[:, m0 // 16 : m1 // 16]), func=ACT.Exp,
                bias=bias[:, t : t + 1], scale=temp_sb[:, t : t + 1],
            )

        e_half(0, 0)
        for t in range(4):
            if t < 3:
                e_half(0, t + 1)
            e_half(1, t)
            nc.vector.tensor_scalar(
                out=bias[:, t : t + 1], in0=top[:, 4 + t : 5 + t], scalar1=temp_sb[:, t : t + 1], scalar2=-1.0,
                op0=ALU.mult, op1=ALU.mult,
            )
            if t < 3:
                look(t, 0, M)

        y = staged([P, 4, M], F32, "y", 7 * SLOT)
        y_bf = kept([P, 4 * M], BF16, "y_bf")
        y_w = kept([P, M], U32, "y_w")
        y_s = kept([P, M], U8, "y_s")
        y_rows = out_0.rearrange("(p t) m -> p t m", t=4)
        words_out = out_1[0].rearrange("p m t -> p (m t)").bitcast(I32)

        def finish_y(t0, t1, m0, m1):
            nc.vector.tensor_tensor(out=y[:, t0:t1, m0:m1], in0=factor[:, t0:t1, m0:m1], in1=a[:, t0:t1, m0:m1], op=ALU.mult)
            nc.sync.dma_start(out=y_rows[:, t0:t1, m0:m1], in_=y[:, t0:t1, m0:m1])

        finish_y(0, 2, 0, M)
        finish_y(2, 3, 0, M)
        for m0 in (0, M // 2):
            m1 = m0 + M // 2
            look(3, m0, m1)
            finish_y(3, 4, m0, m1)
            nc.vector.tensor_copy(
                out=y_bf[:, 4 * m0 : 4 * m1].rearrange("p (c i t) -> p c t i", i=2, t=4),
                in_=y[:, :, m0:m1].rearrange("p t (c i) -> p c t i", i=2),
            )
            nc.vector.quantize_mx(out=y_w[:, m0:m1].bitcast(FP8X4), scales=y_s[:, m0:m1], in_=y_bf[:, 4 * m0 : 4 * m1])
            nc.sync.dma_start(out=words_out[:, m0:m1], in_=y_w[:, m0:m1].bitcast(I32))
        for q in range(4):
            engine = nc.scalar if q % 2 else nc.sync
            engine.dma_start(out=out_2[0, 4 * q : 4 * q + 4, :].bitcast(I32), in_=y_s[32 * q : 32 * q + 4, :].bitcast(I32))
